import numpy as np
import ml_dtypes


def mxq(x, axis, fmt="e4m3"):
    dtype, down = {"e4m3": (ml_dtypes.float8_e4m3fn, 7), "e5m2": (ml_dtypes.float8_e5m2, 14)}[fmt]
    v = np.moveaxis(np.asarray(x, np.float32).astype(ml_dtypes.bfloat16).astype(np.float64), axis, -1)
    blocks = v.reshape(v.shape[:-1] + (-1, 32))
    amax = np.abs(blocks).max(-1, keepdims=True)
    byte = np.maximum(np.where(amax > 0, np.frexp(amax)[1] - 1 + 127, 0) - down, 1)
    scale = np.exp2(byte - 127.0)
    codes = (blocks / scale).astype(np.float32).astype(dtype).astype(np.float64)
    return np.moveaxis((codes * scale).reshape(v.shape), -1, axis)


WIDE = False


def mx_kscale(k):
    if not WIDE:
        return np.ones(k)
    levels = np.array([10, -10, 5, -5, 0])
    if k % 512:
        return np.exp2(np.random.permutation(np.resize(levels, k // 32))).repeat(32)
    a = np.empty((k // 512, 16))
    for p in range(k // 512):
        a[p, :8] = np.random.permutation(np.resize(levels, 8))
        for g in range(8):
            far = levels[np.abs(levels - a[p, g]) >= 10]
            a[p, g + 8] = far[np.random.randint(len(far))]
    return np.exp2(a.ravel()).repeat(32)


def f64(x):
    return np.asarray(x).astype(np.float64)


def striped(idx):
    return np.tile(idx.reshape(-1, 16).T, (8, 1)).astype(np.uint16)


def unstriped(offs):
    return offs[:16].T.reshape(-1).astype(np.int64)


def pack_weight(w):
    k, n = w.shape
    w = f64(np.asarray(w, np.float32).astype(ml_dtypes.bfloat16)).reshape(k // 32, 32, n)
    amax = np.abs(w).max(1)
    byte = np.clip(np.where(amax > 0, np.frexp(amax)[1] - 1 + 127 - 7, 1), 1, 254)
    scaled = (w * np.exp2(127.0 - byte)[:, None, :]).reshape(k, n).astype(np.float32)
    words = np.ascontiguousarray(scaled.reshape(k // 512, 128, 4, n).transpose(0, 1, 3, 2)).astype(ml_dtypes.float8_e4m3fn).view(np.uint8)
    return words, np.ascontiguousarray(byte.astype(np.uint8).reshape(k // 512, 16, n))


def unpack_weight(words, scales):
    g, p, n, _ = words.shape
    vals = np.ascontiguousarray(words).view(ml_dtypes.float8_e4m3fn).astype(np.float64) * np.repeat(np.exp2(scales.astype(np.float64) - 127.0), 8, axis=1)[..., None]
    return vals.transpose(0, 1, 3, 2).reshape(g * 512, n)


def relu(v):
    return np.maximum(v, 0.0)


K, T, S, H, D, W, U = 1024, 2048, 512, 512, 4, 2048, 512


def setup_inputs():
    n = np.random.standard_normal
    s = mx_kscale(K)[:, None]
    u = mx_kscale(H)
    packed_xT = pack_weight(n((K, T)) * s)
    packed_eT = pack_weight(n((H, W)) / np.sqrt(H) / u[:, None])
    return {
        "x_words": packed_xT[0],
        "x_scales": packed_xT[1],
        "w1": (n((K, H)) / np.sqrt(K) / s * u).astype(np.float32),
        "e_words": packed_eT[0],
        "e_scales": packed_eT[1],
        "offs": striped(np.random.permutation(T)[:S]),
        "pos": striped(np.random.permutation(W)[:U]),
        "neg": striped(np.random.permutation(W)[:U]),
    }


def reference(x_words, x_scales, w1, e_words, e_scales, offs, pos, neg):
    xq = unpack_weight(x_words, x_scales)[:, unstriped(offs)]
    h = mxq(f64(w1), 0, "e4m3").T @ xq
    hq = mxq(h, 0, "e4m3")
    e_neg = unpack_weight(e_words, e_scales)[:, unstriped(neg)]
    z = hq.T @ e_neg
    neg1 = z.reshape(len(z), -1, D).max(axis=2)
    e_pos = unpack_weight(e_words, e_scales)[:, unstriped(pos)]
    y = hq.T @ e_pos
    pos1 = y.reshape(len(y), -1, D).min(axis=2)
    return relu(neg1 - pos1 + 0.3)

@@ -1,0 +1,173 @@
+from contextlib import ExitStack
+
+import concourse.mybir as mybir
+
+K, T, S, H, D, U = 1024, 2048, 512, 512, 4, 512
+FLOPS = 2 * K * H * S + 2 * 2 * H * S * U
+
+F32 = mybir.dt.float32
+BF16 = mybir.dt.bfloat16
+I32 = mybir.dt.int32
+U32 = mybir.dt.uint32
+U16 = mybir.dt.uint16
+U8 = mybir.dt.uint8
+FP8X4 = mybir.dt.float8_e4m3fn_x4
+ALU = mybir.AluOpType
+ACT = mybir.ActivationFunctionType
+
+P = 128
+PACK = 4
+PASSES = K // (P * PACK)
+TOK = 128
+TILES = S // TOK
+V = U // D
+E_ROW = 8
+MARGIN = 0.3
+
+
+def tile_picked_yhard_hinge_p_kernel(tc, x_words, x_scales, w1, e_words, e_scales, offs, pos, neg, out):
+    nc = tc.nc
+    with ExitStack() as ctx:
+        lists = ctx.enter_context(tc.tile_pool(name="lists", bufs=1))
+        keep = ctx.enter_context(tc.tile_pool(name="keep", bufs=1))
+        h_psum = ctx.enter_context(tc.psum_pool(name="h_psum", bufs=3))
+        s_psum = ctx.enter_context(tc.psum_pool(name="s_psum", bufs=5))
+
+        offs_t = lists.tile([P, S // 16], U16, name="offs_t")
+        neg_t = lists.tile([P, U // 16], U16, name="neg_t")
+        pos_t = lists.tile([P, U // 16], U16, name="pos_t")
+
+        xs_all = keep.tile([P, T], U8, name="xs_all", tag="xs_then_ws", align_bytes=64)
+        es_all = keep.tile([P, T], U8, name="es_all", align_bytes=64)
+        nc.vector.memset(es_all[:].bitcast(I32), 0)
+        nc.gpsimd.memset(xs_all[:].bitcast(I32), 0)
+
+        w_raw = [keep.tile([P, PACK, H], F32, name="w_raw%d" % o) for o in range(PASSES)]
+        xw_all = [keep.tile([P, T], I32, name="xw_all%d" % o, tag="xw%d" % o, align_bytes=64) for o in range(PASSES)]
+        ew_all = keep.tile([P, T], I32, name="ew_all", tag="e_then_h", align_bytes=64)
+
+        def load_w(o):
+            nc.sync.dma_start(out=w_raw[o][:], in_=w1[512 * o : 512 * (o + 1), :].rearrange("(p j) c -> p j c", j=PACK))
+
+        nc.sync.dma_start(neg_t[:], neg)
+        load_w(0)
+        nc.sync.dma_start(offs_t[:], offs)
+        nc.sync.dma_start(pos_t[:], pos)
+        for q in range(4):
+            nc.sync.dma_start(out=es_all[32 * q + E_ROW : 32 * q + E_ROW + 4, :].bitcast(I32), in_=e_scales[0, 4 * q : 4 * q + 4, :].bitcast(I32))
+        load_w(1)
+        for q in range(4):
+            nc.sync.dma_start(out=xs_all[32 * q : 32 * q + 4 * PASSES, :].bitcast(I32), in_=x_scales[:, 4 * q : 4 * q + 4, :].bitcast(I32))
+        for o in range(PASSES):
+            nc.sync.dma_start(out=xw_all[o][:], in_=x_words[o].rearrange("p n t -> p (n t)").bitcast(I32))
+        nc.sync.dma_start(out=ew_all[:], in_=e_words[0].rearrange("p n t -> p (n t)").bitcast(I32))
+
+        w_bf = [keep.tile([P, PACK, P, PACK], BF16, name="w_bf%d" % o, align_bytes=64) for o in range(PASSES)]
+        w_q = []
+        w_s = []
+        for o in range(PASSES):
+            nc.scalar.activation(
+                out=w_bf[o][:].rearrange("p t m j -> p m j t"),
+                in_=w_raw[o][:].rearrange("p j (m t) -> p m j t", t=PACK),
+                func=ACT.Copy,
+            )
+
+        def quantize_w(o, codes_tag, scales_tag):
+            w_q.append(keep.tile([P, H], U32, name="w_q%d" % o, tag=codes_tag, align_bytes=64))
+            w_s.append(keep.tile([P, H], U8, name="w_s%d" % o, tag=scales_tag, align_bytes=64))
+            nc.vector.quantize_mx(out=w_q[o][:].bitcast(FP8X4), scales=w_s[o][:], in_=w_bf[o][:].rearrange("p t m j -> p (t m j)"))
+
+        xs_g = keep.tile([P, S], U8, name="xs_g", align_bytes=64)
+        ns_g = keep.tile([P, U], U8, name="ns_g", align_bytes=64)
+        ps_g = keep.tile([P, U], U8, name="ps_g", align_bytes=64)
+        nc.vector.tensor_copy(ns_g[:], es_all[:].indirect(neg_t[:]))
+        nc.vector.tensor_copy(ps_g[:], es_all[:].indirect(pos_t[:]))
+        quantize_w(0, "wq0", "ws0")
+        nc.vector.tensor_copy(xs_g[:], xs_all[:].indirect(offs_t[:]))
+        xw_g = [keep.tile([P, S], U32, name="xw_g%d" % o, align_bytes=64) for o in range(PASSES)]
+        nc.vector.tensor_copy(xw_g[0][:], xw_all[0][:].bitcast(U32).indirect(offs_t[:]))
+        quantize_w(1, "xw0", "xs_then_ws")
+        for half in range(2):
+            nc.vector.tensor_copy(
+                xw_g[1][:, 256 * half : 256 * (half + 1)],
+                xw_all[1][:].bitcast(U32).indirect(offs_t[:, 16 * half : 16 * (half + 1)]),
+            )
+
+        h_bf = []
+        for i in range(TILES):
+            tok = slice(TOK * i, TOK * (i + 1))
+            h_acc = h_psum.tile([P, PACK, TOK], F32, name="h_acc")
+            for t in range(PACK):
+                ch = slice(P * t, P * (t + 1))
+                for o in range(PASSES):
+                    nc.tensor.matmul_mx(
+                        out=h_acc[:, t, :],
+                        lhsT=w_q[o][:, ch].bitcast(FP8X4),
+                        lhsT_scale=w_s[o][:, ch],
+                        rhs=xw_g[o][:, tok].bitcast(FP8X4),
+                        rhs_scale=xs_g[4 * o : P, tok],
+                        start=(o == 0),
+                        stop=(o == PASSES - 1),
+                    )
+            hb = keep.tile([P, TOK, PACK], BF16, name="h_bf%d" % i, align_bytes=64)
+            nc.scalar.copy(out=hb[:], in_=h_acc[:].rearrange("p t n -> p n t"))
+            h_bf.append(hb)
+
+        h_q = []
+        h_s = [keep.tile([P, TOK], U8, name="h_s%d" % i, align_bytes=64) for i in range(TILES)]
+
+        def quantize_h(i):
+            nc.vector.quantize_mx(out=h_q[i].bitcast(FP8X4), scales=h_s[i][:], in_=h_bf[i][:].rearrange("p n t -> p (n t)"))
+
+        nw_g = keep.tile([P, U], U32, name="nw_g", align_bytes=64)
+        pw_g = keep.tile([P, U], U32, name="pw_g", align_bytes=64)
+        nc.vector.tensor_copy(nw_g[:], ew_all[:].bitcast(U32).indirect(neg_t[:]))
+        nc.vector.tensor_copy(pw_g[:], ew_all[:].bitcast(U32).indirect(pos_t[:]))
+        h_late = keep.tile([P, TILES * TOK], U32, name="h_late", tag="e_then_h", align_bytes=64)
+        for i in range(TILES):
+            h_q.append(h_late[:, TOK * i : TOK * (i + 1)])
+            quantize_h(i)
+
+        jobs = [(i, nw_g, ns_g, ALU.max) for i in range(TILES)] + [(i, pw_g, ps_g, ALU.min) for i in range(TILES)]
+        pairs = {}
+        best = {}
+
+        def first_round(n):
+            i, words, scales, op = jobs[n]
+            acc = s_psum.tile([P, V, D], F32, name="s_acc")
+            nc.tensor.matmul_mx(
+                out=acc[:].rearrange("p v d -> p (v d)"),
+                lhsT=h_q[i].bitcast(FP8X4),
+                lhsT_scale=h_s[i][:],
+                rhs=words[:].bitcast(FP8X4),
+                rhs_scale=scales[E_ROW:P, :],
+                start=True,
+                stop=True,
+            )
+            if n == 0:
+                best[n] = keep.tile([P, V], F32, name="best%d" % n)
+                nc.vector.tensor_reduce(out=best[n][:], in_=acc[:], axis=mybir.AxisListType.X, op=op)
+                return
+            upper = keep.tile([P, V, 2], F32, name="upper%d" % n)
+            nc.scalar.copy(out=upper[:], in_=acc[:, :, 2:4])
+            pairs[n] = keep.tile([P, V, 2], F32, name="pair%d" % n)
+            nc.vector.tensor_tensor(out=pairs[n][:], in0=acc[:, :, 0:2], in1=upper[:], op=op)
+
+        def second_round(n):
+            best[n] = keep.tile([P, V], F32, name="best%d" % n)
+            nc.vector.tensor_tensor(out=best[n][:], in0=pairs[n][:, :, 0], in1=pairs[n][:, :, 1], op=jobs[n][3])
+
+        def finish(i):
+            gap = keep.tile([P, V], F32, name="gap%d" % i)
+            nc.vector.scalar_tensor_tensor(out=gap[:], in0=best[i][:], scalar=MARGIN, in1=best[TILES + i][:], op0=ALU.add, op1=ALU.subtract)
+            loss = keep.tile([P, V], F32, name="loss%d" % i)
+            nc.scalar.activation(out=loss[:], in_=gap[:], func=ACT.Relu)
+            nc.sync.dma_start(out=out[TOK * i : TOK * (i + 1), :], in_=loss[:])
+
+        for n in range(len(jobs) + 2):
+            if n < len(jobs):
+                first_round(n)
+            if 2 <= n <= len(jobs):
+                second_round(n - 1)
+            if n - 2 >= TILES:
+                finish(n - 2 - TILES)

@@ -53,10 +53,10 @@ def tile_picked_yhard_hinge_p_kernel(tc, x_words, x_scales, w1, e_words, e_scale
         load_w(0)
         nc.sync.dma_start(offs_t[:], offs)
         nc.sync.dma_start(pos_t[:], pos)
-        for q in range(4):
-            nc.sync.dma_start(out=es_all[32 * q + E_ROW : 32 * q + E_ROW + 4, :].bitcast(I32), in_=e_scales[0, 4 * q : 4 * q + 4, :].bitcast(I32))
+        for r in range(4):
+            nc.sync.dma_start(out=es_all[E_ROW + r : P : 32, :].bitcast(I32), in_=e_scales[0, r:16:4, :].bitcast(I32))
         load_w(1)
-        for q in range(4):
+        for q in (0, 2, 1, 3):
             nc.sync.dma_start(out=xs_all[32 * q : 32 * q + 4 * PASSES, :].bitcast(I32), in_=x_scales[:, 4 * q : 4 * q + 4, :].bitcast(I32))
         for o in range(PASSES):
             nc.sync.dma_start(out=xw_all[o][:], in_=x_words[o].rearrange("p n t -> p (n t)").bitcast(I32))
@@ -67,8 +67,8 @@ def tile_picked_yhard_hinge_p_kernel(tc, x_words, x_scales, w1, e_words, e_scale
         w_s = []
         for o in range(PASSES):
             nc.scalar.activation(
-                out=w_bf[o][:].rearrange("p t m j -> p m j t"),
-                in_=w_raw[o][:].rearrange("p j (m t) -> p m j t", t=PACK),
+                out=w_bf[o][:].rearrange("p t m j -> p m t j"),
+                in_=w_raw[o][:].rearrange("p j (m t) -> p m t j", t=PACK),
                 func=ACT.Copy,
             )
 

@@ -21,7 +21,6 @@ PASSES = K // (P * PACK)
 TOK = 128
 TILES = S // TOK
 V = U // D
-E_ROW = 8
 MARGIN = 0.3
 
 
@@ -37,30 +36,50 @@ def tile_picked_yhard_hinge_p_kernel(tc, x_words, x_scales, w1, e_words, e_scale
         neg_t = lists.tile([P, U // 16], U16, name="neg_t")
         pos_t = lists.tile([P, U // 16], U16, name="pos_t")
 
-        xs_all = keep.tile([P, T], U8, name="xs_all", tag="xs_then_ws", align_bytes=64)
-        es_all = keep.tile([P, T], U8, name="es_all", align_bytes=64)
+        xs_all = keep.tile([P, T], U8, name="xs_all", tag="xs_then_x1", align_bytes=64)
+        es_all = keep.tile([P, T], U8, name="es_all", tag="es_then_e", align_bytes=64)
+        planes = keep.tile([P, 4, S], U8, name="planes", align_bytes=64)
+        nc.vector.memset(xs_all[:].bitcast(I32), 0)
         nc.vector.memset(es_all[:].bitcast(I32), 0)
-        nc.gpsimd.memset(xs_all[:].bitcast(I32), 0)
+        nc.vector.memset(planes[:].rearrange("p a n -> p (a n)").bitcast(I32), 0)
 
         w_raw = [keep.tile([P, PACK, H], F32, name="w_raw%d" % o) for o in range(PASSES)]
-        xw_all = [keep.tile([P, T], I32, name="xw_all%d" % o, tag="xw%d" % o, align_bytes=64) for o in range(PASSES)]
-        ew_all = keep.tile([P, T], I32, name="ew_all", tag="e_then_h", align_bytes=64)
 
         def load_w(o):
             nc.sync.dma_start(out=w_raw[o][:], in_=w1[512 * o : 512 * (o + 1), :].rearrange("(p j) c -> p j c", j=PACK))
 
-        nc.sync.dma_start(neg_t[:], neg)
+        def load_words(tile, words):
+            nc.sync.dma_start(out=tile[:], in_=words.rearrange("p n t -> p (n t)").bitcast(I32))
+
         load_w(0)
         nc.sync.dma_start(offs_t[:], offs)
+        nc.sync.dma_start(out=xs_all[0:P:4, :].bitcast(I32), in_=x_scales.rearrange("o q c -> q o c").bitcast(I32))
+        nc.sync.dma_start(neg_t[:], neg)
+        nc.sync.dma_start(out=es_all[0:P:8, :].bitcast(I32), in_=e_scales[0].bitcast(I32))
         nc.sync.dma_start(pos_t[:], pos)
-        for r in range(4):
-            nc.sync.dma_start(out=es_all[E_ROW + r : P : 32, :].bitcast(I32), in_=e_scales[0, r:16:4, :].bitcast(I32))
         load_w(1)
-        for q in (0, 2, 1, 3):
-            nc.sync.dma_start(out=xs_all[32 * q : 32 * q + 4 * PASSES, :].bitcast(I32), in_=x_scales[:, 4 * q : 4 * q + 4, :].bitcast(I32))
-        for o in range(PASSES):
-            nc.sync.dma_start(out=xw_all[o][:], in_=x_words[o].rearrange("p n t -> p (n t)").bitcast(I32))
-        nc.sync.dma_start(out=ew_all[:], in_=e_words[0].rearrange("p n t -> p (n t)").bitcast(I32))
+        xw_all = [keep.tile([P, T], I32, name="xw_all0", tag="xw0", align_bytes=64)]
+        load_words(xw_all[0], x_words[0])
+
+        xs_g = keep.tile([P, S], U8, name="xs_g", align_bytes=64)
+        es_g = keep.tile([P, 2, U], U8, name="es_g", align_bytes=64)
+        nc.vector.tensor_copy(xs_g[:], xs_all[:].indirect(offs_t[:]))
+        for q in range(4):
+            nc.sync.dma_start(
+                out=planes[32 * q : 32 * q + 4, 0:2, :].rearrange("p a n -> p (a n)").bitcast(I32),
+                in_=xs_g[32 * q : 32 * q + 32 : 4, :].bitcast(I32),
+            )
+        xw_all.append(keep.tile([P, T], I32, name="xw_all1", tag="xs_then_x1", align_bytes=64))
+        load_words(xw_all[1], x_words[1])
+        nc.vector.tensor_copy(es_g[:, 0, :], es_all[:].indirect(neg_t[:]))
+        nc.vector.tensor_copy(es_g[:, 1, :], es_all[:].indirect(pos_t[:]))
+        ew_all = keep.tile([P, T], I32, name="ew_all", tag="es_then_e", align_bytes=64)
+        load_words(ew_all, e_words[0])
+        for q in range(4):
+            nc.sync.dma_start(
+                out=planes[32 * q : 32 * q + 4, 2:4, :].rearrange("p a n -> p (a n)").bitcast(I32),
+                in_=es_g[32 * q : 32 * q + 32 : 8, :, :].rearrange("p a n -> p (a n)").bitcast(I32),
+            )
 
         w_bf = [keep.tile([P, PACK, P, PACK], BF16, name="w_bf%d" % o, align_bytes=64) for o in range(PASSES)]
         w_q = []
@@ -77,16 +96,10 @@ def tile_picked_yhard_hinge_p_kernel(tc, x_words, x_scales, w1, e_words, e_scale
             w_s.append(keep.tile([P, H], U8, name="w_s%d" % o, tag=scales_tag, align_bytes=64))
             nc.vector.quantize_mx(out=w_q[o][:].bitcast(FP8X4), scales=w_s[o][:], in_=w_bf[o][:].rearrange("p t m j -> p (t m j)"))
 
-        xs_g = keep.tile([P, S], U8, name="xs_g", align_bytes=64)
-        ns_g = keep.tile([P, U], U8, name="ns_g", align_bytes=64)
-        ps_g = keep.tile([P, U], U8, name="ps_g", align_bytes=64)
-        nc.vector.tensor_copy(ns_g[:], es_all[:].indirect(neg_t[:]))
-        nc.vector.tensor_copy(ps_g[:], es_all[:].indirect(pos_t[:]))
         quantize_w(0, "wq0", "ws0")
-        nc.vector.tensor_copy(xs_g[:], xs_all[:].indirect(offs_t[:]))
         xw_g = [keep.tile([P, S], U32, name="xw_g%d" % o, align_bytes=64) for o in range(PASSES)]
         nc.vector.tensor_copy(xw_g[0][:], xw_all[0][:].bitcast(U32).indirect(offs_t[:]))
-        quantize_w(1, "xw0", "xs_then_ws")
+        quantize_w(1, "xw0", "ws1")
         for half in range(2):
             nc.vector.tensor_copy(
                 xw_g[1][:, 256 * half : 256 * (half + 1)],
@@ -105,7 +118,7 @@ def tile_picked_yhard_hinge_p_kernel(tc, x_words, x_scales, w1, e_words, e_scale
                         lhsT=w_q[o][:, ch].bitcast(FP8X4),
                         lhsT_scale=w_s[o][:, ch],
                         rhs=xw_g[o][:, tok].bitcast(FP8X4),
-                        rhs_scale=xs_g[4 * o : P, tok],
+                        rhs_scale=planes[:, o, tok],
                         start=(o == 0),
                         stop=(o == PASSES - 1),
                     )
@@ -123,12 +136,12 @@ def tile_picked_yhard_hinge_p_kernel(tc, x_words, x_scales, w1, e_words, e_scale
         pw_g = keep.tile([P, U], U32, name="pw_g", align_bytes=64)
         nc.vector.tensor_copy(nw_g[:], ew_all[:].bitcast(U32).indirect(neg_t[:]))
         nc.vector.tensor_copy(pw_g[:], ew_all[:].bitcast(U32).indirect(pos_t[:]))
-        h_late = keep.tile([P, TILES * TOK], U32, name="h_late", tag="e_then_h", align_bytes=64)
+        h_late = keep.tile([P, TILES * TOK], U32, name="h_late", tag="es_then_e", align_bytes=64)
         for i in range(TILES):
             h_q.append(h_late[:, TOK * i : TOK * (i + 1)])
             quantize_h(i)
 
-        jobs = [(i, nw_g, ns_g, ALU.max) for i in range(TILES)] + [(i, pw_g, ps_g, ALU.min) for i in range(TILES)]
+        jobs = [(i, nw_g, 2, ALU.max) for i in range(TILES)] + [(i, pw_g, 3, ALU.min) for i in range(TILES)]
         pairs = {}
         best = {}
 
@@ -140,7 +153,7 @@ def tile_picked_yhard_hinge_p_kernel(tc, x_words, x_scales, w1, e_words, e_scale
                 lhsT=h_q[i].bitcast(FP8X4),
                 lhsT_scale=h_s[i][:],
                 rhs=words[:].bitcast(FP8X4),
-                rhs_scale=scales[E_ROW:P, :],
+                rhs_scale=planes[:, scales, :],
                 start=True,
                 stop=True,
             )

@@ -29,8 +29,7 @@ def tile_picked_yhard_hinge_p_kernel(tc, x_words, x_scales, w1, e_words, e_scale
     with ExitStack() as ctx:
         lists = ctx.enter_context(tc.tile_pool(name="lists", bufs=1))
         keep = ctx.enter_context(tc.tile_pool(name="keep", bufs=1))
-        h_psum = ctx.enter_context(tc.psum_pool(name="h_psum", bufs=3))
-        s_psum = ctx.enter_context(tc.psum_pool(name="s_psum", bufs=5))
+        psum = ctx.enter_context(tc.psum_pool(name="psum", bufs=8))
 
         offs_t = lists.tile([P, S // 16], U16, name="offs_t")
         neg_t = lists.tile([P, U // 16], U16, name="neg_t")
@@ -62,7 +61,7 @@ def tile_picked_yhard_hinge_p_kernel(tc, x_words, x_scales, w1, e_words, e_scale
         load_words(xw_all[0], x_words[0])
 
         xs_g = keep.tile([P, S], U8, name="xs_g", align_bytes=64)
-        es_g = keep.tile([P, 2, U], U8, name="es_g", align_bytes=64)
+        es_g = keep.tile([P, 2, U], U8, name="es_g", tag="es_g_then_hs", align_bytes=64)
         nc.vector.tensor_copy(xs_g[:], xs_all[:].indirect(offs_t[:]))
         for q in range(4):
             nc.sync.dma_start(
@@ -109,7 +108,7 @@ def tile_picked_yhard_hinge_p_kernel(tc, x_words, x_scales, w1, e_words, e_scale
         h_bf = []
         for i in range(TILES):
             tok = slice(TOK * i, TOK * (i + 1))
-            h_acc = h_psum.tile([P, PACK, TOK], F32, name="h_acc")
+            h_acc = psum.tile([P, PACK, TOK], F32, name="h_acc", tag="bank")
             for t in range(PACK):
                 ch = slice(P * t, P * (t + 1))
                 for o in range(PASSES):
@@ -122,65 +121,78 @@ def tile_picked_yhard_hinge_p_kernel(tc, x_words, x_scales, w1, e_words, e_scale
                         start=(o == 0),
                         stop=(o == PASSES - 1),
                     )
-            hb = keep.tile([P, TOK, PACK], BF16, name="h_bf%d" % i, align_bytes=64)
+            hb = keep.tile([P, TOK, PACK], BF16, name="h_bf%d" % i, tag="h_bf%d" % i, align_bytes=64)
             nc.scalar.copy(out=hb[:], in_=h_acc[:].rearrange("p t n -> p n t"))
             h_bf.append(hb)
 
-        h_q = []
-        h_s = [keep.tile([P, TOK], U8, name="h_s%d" % i, align_bytes=64) for i in range(TILES)]
+        h_q = [keep.tile([P, TOK], U32, name="h_q0", align_bytes=64)[:]]
+        h_s = keep.tile([P, S], U8, name="h_s", tag="es_g_then_hs", align_bytes=64)
 
         def quantize_h(i):
-            nc.vector.quantize_mx(out=h_q[i].bitcast(FP8X4), scales=h_s[i][:], in_=h_bf[i][:].rearrange("p n t -> p (n t)"))
+            tok = slice(TOK * i, TOK * (i + 1))
+            nc.vector.quantize_mx(out=h_q[i].bitcast(FP8X4), scales=h_s[:, tok], in_=h_bf[i][:].rearrange("p n t -> p (n t)"))
 
         nw_g = keep.tile([P, U], U32, name="nw_g", align_bytes=64)
-        pw_g = keep.tile([P, U], U32, name="pw_g", align_bytes=64)
         nc.vector.tensor_copy(nw_g[:], ew_all[:].bitcast(U32).indirect(neg_t[:]))
+        quantize_h(0)
+        pw_g = keep.tile([P, U], U32, name="pw_g", tag="h_bf0", align_bytes=64)
         nc.vector.tensor_copy(pw_g[:], ew_all[:].bitcast(U32).indirect(pos_t[:]))
-        h_late = keep.tile([P, TILES * TOK], U32, name="h_late", tag="es_then_e", align_bytes=64)
-        for i in range(TILES):
-            h_q.append(h_late[:, TOK * i : TOK * (i + 1)])
+
+        h_late = keep.tile([P, S - TOK], U32, name="h_late", tag="es_then_e", align_bytes=64)
+        for i in range(1, TILES):
+            h_q.append(h_late[:, TOK * (i - 1) : TOK * i])
             quantize_h(i)
 
-        jobs = [(i, nw_g, 2, ALU.max) for i in range(TILES)] + [(i, pw_g, 3, ALU.min) for i in range(TILES)]
-        pairs = {}
-        best = {}
+        sides = ((nw_g, 2, 1.0), (pw_g, 3, -1.0))
+        pairs = keep.tile([P, TILES, 2, 2, V], F32, name="pairs")
+        best = keep.tile([P, TILES, 2, V], F32, name="best")
+        gap = keep.tile([P, TILES, V], F32, name="gap")
+        loss = keep.tile([P, TILES, V], F32, name="loss")
 
-        def first_round(n):
-            i, words, scales, op = jobs[n]
-            acc = s_psum.tile([P, V, D], F32, name="s_acc")
+        def first_round(i, side):
+            words, plane, sign = sides[side]
+            tok = slice(TOK * i, TOK * (i + 1))
+            acc = psum.tile([P, V, D], F32, name="s_acc", tag="bank")
             nc.tensor.matmul_mx(
                 out=acc[:].rearrange("p v d -> p (v d)"),
                 lhsT=h_q[i].bitcast(FP8X4),
-                lhsT_scale=h_s[i][:],
+                lhsT_scale=h_s[:, tok],
                 rhs=words[:].bitcast(FP8X4),
-                rhs_scale=planes[:, scales, :],
+                rhs_scale=planes[:, plane, :],
                 start=True,
                 stop=True,
             )
-            if n == 0:
-                best[n] = keep.tile([P, V], F32, name="best%d" % n)
-                nc.vector.tensor_reduce(out=best[n][:], in_=acc[:], axis=mybir.AxisListType.X, op=op)
-                return
-            upper = keep.tile([P, V, 2], F32, name="upper%d" % n)
-            nc.scalar.copy(out=upper[:], in_=acc[:, :, 2:4])
-            pairs[n] = keep.tile([P, V, 2], F32, name="pair%d" % n)
-            nc.vector.tensor_tensor(out=pairs[n][:], in0=acc[:, :, 0:2], in1=upper[:], op=op)
+            by_entry = acc[:].rearrange("p v d -> p d v")
+            upper = keep.tile([P, 2, V], F32, name="upper%d_%d" % (i, side), tag="upper%d_%d" % (i, side))
+            nc.scalar.activation(out=upper[:], in_=by_entry[:, 2:4], func=ACT.Copy, scale=sign)
+            nc.vector.scalar_tensor_tensor(out=pairs[:, i, side], in0=by_entry[:, 0:2], scalar=sign, in1=upper[:], op0=ALU.mult, op1=ALU.max)
 
-        def second_round(n):
-            best[n] = keep.tile([P, V], F32, name="best%d" % n)
-            nc.vector.tensor_tensor(out=best[n][:], in0=pairs[n][:, :, 0], in1=pairs[n][:, :, 1], op=jobs[n][3])
+        def second_round(lo, hi):
+            both = pairs[:, lo:hi].rearrange("p i s d v -> p (i s) d v")
+            nc.vector.tensor_tensor(out=best[:, lo:hi].rearrange("p i s v -> p (i s) v"), in0=both[:, :, 0], in1=both[:, :, 1], op=ALU.max)
 
-        def finish(i):
-            gap = keep.tile([P, V], F32, name="gap%d" % i)
-            nc.vector.scalar_tensor_tensor(out=gap[:], in0=best[i][:], scalar=MARGIN, in1=best[TILES + i][:], op0=ALU.add, op1=ALU.subtract)
-            loss = keep.tile([P, V], F32, name="loss%d" % i)
-            nc.scalar.activation(out=loss[:], in_=gap[:], func=ACT.Relu)
-            nc.sync.dma_start(out=out[TOK * i : TOK * (i + 1), :], in_=loss[:])
+        def difference(lo, hi, engine):
+            engine.tensor_tensor(out=gap[:, lo:hi], in0=best[:, lo:hi, 0], in1=best[:, lo:hi, 1], op=ALU.add)
 
-        for n in range(len(jobs) + 2):
-            if n < len(jobs):
-                first_round(n)
-            if 2 <= n <= len(jobs):
-                second_round(n - 1)
-            if n - 2 >= TILES:
-                finish(n - 2 - TILES)
+        def hinge_on_vector(i):
+            nc.vector.tensor_scalar(out=loss[:, i], in0=gap[:, i], scalar1=MARGIN, scalar2=0.0, op0=ALU.add, op1=ALU.max)
+            nc.sync.dma_start(out=out[TOK * i : TOK * (i + 1), :], in_=loss[:, i])
+
+        for i in range(2):
+            first_round(i, 0)
+            first_round(i, 1)
+        first_round(2, 0)
+        second_round(0, 2)
+        difference(0, 2, nc.gpsimd)
+        first_round(2, 1)
+        first_round(3, 0)
+        first_round(3, 1)
+        early = keep.tile([P, 2, V], F32, name="early", tag="upper3_0")
+        nc.scalar.activation(out=early[:], in_=gap[:, 0:2], func=ACT.Relu, bias=MARGIN)
+        nc.sync.dma_start(out=out[0 : 2 * TOK, :].rearrange("(i p) v -> p i v", p=TOK), in_=early[:])
+        second_round(2, 3)
+        second_round(3, 4)
+        difference(2, 3, nc.vector)
+        difference(3, 4, nc.vector)
+        hinge_on_vector(2)
+        hinge_on_vector(3)

@@ -22,6 +22,7 @@ TOK = 128
 TILES = S // TOK
 V = U // D
 MARGIN = 0.3
+EARLY = 2
 
 
 def tile_picked_yhard_hinge_p_kernel(tc, x_words, x_scales, w1, e_words, e_scales, offs, pos, neg, out):
@@ -35,8 +36,8 @@ def tile_picked_yhard_hinge_p_kernel(tc, x_words, x_scales, w1, e_words, e_scale
         neg_t = lists.tile([P, U // 16], U16, name="neg_t")
         pos_t = lists.tile([P, U // 16], U16, name="pos_t")
 
-        xs_all = keep.tile([P, T], U8, name="xs_all", tag="xs_then_x1", align_bytes=64)
-        es_all = keep.tile([P, T], U8, name="es_all", tag="es_then_e", align_bytes=64)
+        xs_all = keep.tile([P, T], U8, name="xs_all", tag="xs_then_e", align_bytes=64)
+        es_all = keep.tile([P, T], U8, name="es_all", align_bytes=64)
         planes = keep.tile([P, 4, S], U8, name="planes", align_bytes=64)
         nc.vector.memset(xs_all[:].bitcast(I32), 0)
         nc.vector.memset(es_all[:].bitcast(I32), 0)
@@ -57,8 +58,9 @@ def tile_picked_yhard_hinge_p_kernel(tc, x_words, x_scales, w1, e_words, e_scale
         nc.sync.dma_start(out=es_all[0:P:8, :].bitcast(I32), in_=e_scales[0].bitcast(I32))
         nc.sync.dma_start(pos_t[:], pos)
         load_w(1)
-        xw_all = [keep.tile([P, T], I32, name="xw_all0", tag="xw0", align_bytes=64)]
-        load_words(xw_all[0], x_words[0])
+        xw_all = [keep.tile([P, T], I32, name="xw_all%d" % o, tag="xw%d" % o, align_bytes=64) for o in range(PASSES)]
+        for o in range(PASSES):
+            load_words(xw_all[o], x_words[o])
 
         xs_g = keep.tile([P, S], U8, name="xs_g", align_bytes=64)
         es_g = keep.tile([P, 2, U], U8, name="es_g", tag="es_g_then_hs", align_bytes=64)
@@ -68,12 +70,10 @@ def tile_picked_yhard_hinge_p_kernel(tc, x_words, x_scales, w1, e_words, e_scale
                 out=planes[32 * q : 32 * q + 4, 0:2, :].rearrange("p a n -> p (a n)").bitcast(I32),
                 in_=xs_g[32 * q : 32 * q + 32 : 4, :].bitcast(I32),
             )
-        xw_all.append(keep.tile([P, T], I32, name="xw_all1", tag="xs_then_x1", align_bytes=64))
-        load_words(xw_all[1], x_words[1])
+        ew_all = keep.tile([P, T], I32, name="ew_all", tag="xs_then_e", align_bytes=64)
+        load_words(ew_all, e_words[0])
         nc.vector.tensor_copy(es_g[:, 0, :], es_all[:].indirect(neg_t[:]))
         nc.vector.tensor_copy(es_g[:, 1, :], es_all[:].indirect(pos_t[:]))
-        ew_all = keep.tile([P, T], I32, name="ew_all", tag="es_then_e", align_bytes=64)
-        load_words(ew_all, e_words[0])
         for q in range(4):
             nc.sync.dma_start(
                 out=planes[32 * q : 32 * q + 4, 2:4, :].rearrange("p a n -> p (a n)").bitcast(I32),
@@ -105,6 +105,18 @@ def tile_picked_yhard_hinge_p_kernel(tc, x_words, x_scales, w1, e_words, e_scale
                 xw_all[1][:].bitcast(U32).indirect(offs_t[:, 16 * half : 16 * (half + 1)]),
             )
 
+        for t in range(4):
+            idle = psum.tile([P, S], F32, name="idle", tag="bank")
+            nc.tensor.matmul_mx(
+                out=idle[:],
+                lhsT=w_q[0][:, P * t : P * (t + 1)].bitcast(FP8X4),
+                lhsT_scale=w_s[0][:, P * t : P * (t + 1)],
+                rhs=w_q[0][:].bitcast(FP8X4),
+                rhs_scale=w_s[0][:],
+                start=True,
+                stop=True,
+            )
+
         h_bf = []
         for i in range(TILES):
             tok = slice(TOK * i, TOK * (i + 1))
@@ -125,7 +137,8 @@ def tile_picked_yhard_hinge_p_kernel(tc, x_words, x_scales, w1, e_words, e_scale
             nc.scalar.copy(out=hb[:], in_=h_acc[:].rearrange("p t n -> p n t"))
             h_bf.append(hb)
 
-        h_q = [keep.tile([P, TOK], U32, name="h_q0", align_bytes=64)[:]]
+        h_early = keep.tile([P, EARLY * TOK], U32, name="h_early", align_bytes=64)
+        h_q = [h_early[:, TOK * i : TOK * (i + 1)] for i in range(EARLY)]
         h_s = keep.tile([P, S], U8, name="h_s", tag="es_g_then_hs", align_bytes=64)
 
         def quantize_h(i):
@@ -134,13 +147,14 @@ def tile_picked_yhard_hinge_p_kernel(tc, x_words, x_scales, w1, e_words, e_scale
 
         nw_g = keep.tile([P, U], U32, name="nw_g", align_bytes=64)
         nc.vector.tensor_copy(nw_g[:], ew_all[:].bitcast(U32).indirect(neg_t[:]))
-        quantize_h(0)
-        pw_g = keep.tile([P, U], U32, name="pw_g", tag="h_bf0", align_bytes=64)
+        for i in range(EARLY):
+            quantize_h(i)
+        pw_g = keep.tile([P, U], U32, name="pw_g", tag="h_bf%d" % (EARLY - 1), align_bytes=64)
         nc.vector.tensor_copy(pw_g[:], ew_all[:].bitcast(U32).indirect(pos_t[:]))
 
-        h_late = keep.tile([P, S - TOK], U32, name="h_late", tag="es_then_e", align_bytes=64)
-        for i in range(1, TILES):
-            h_q.append(h_late[:, TOK * (i - 1) : TOK * i])
+        h_late = keep.tile([P, S - EARLY * TOK], U32, name="h_late", tag="xs_then_e", align_bytes=64)
+        for i in range(EARLY, TILES):
+            h_q.append(h_late[:, TOK * (i - EARLY) : TOK * (i - EARLY + 1)])
             quantize_h(i)
 
         sides = ((nw_g, 2, 1.0), (pw_g, 3, -1.0))
@@ -178,9 +192,9 @@ def tile_picked_yhard_hinge_p_kernel(tc, x_words, x_scales, w1, e_words, e_scale
             nc.vector.tensor_scalar(out=loss[:, i], in0=gap[:, i], scalar1=MARGIN, scalar2=0.0, op0=ALU.add, op1=ALU.max)
             nc.sync.dma_start(out=out[TOK * i : TOK * (i + 1), :], in_=loss[:, i])
 
-        for i in range(2):
-            first_round(i, 0)
-            first_round(i, 1)
+        for side in range(2):
+            for i in range(2):
+                first_round(i, side)
         first_round(2, 0)
         second_round(0, 2)
         difference(0, 2, nc.gpsimd)

@@ -56,11 +56,10 @@ def tile_picked_yhard_hinge_p_kernel(tc, x_words, x_scales, w1, e_words, e_scale
         nc.sync.dma_start(out=xs_all[0:P:4, :].bitcast(I32), in_=x_scales.rearrange("o q c -> q o c").bitcast(I32))
         nc.sync.dma_start(neg_t[:], neg)
         nc.sync.dma_start(out=es_all[0:P:8, :].bitcast(I32), in_=e_scales[0].bitcast(I32))
-        nc.sync.dma_start(pos_t[:], pos)
         load_w(1)
+        nc.sync.dma_start(pos_t[:], pos)
         xw_all = [keep.tile([P, T], I32, name="xw_all%d" % o, tag="xw%d" % o, align_bytes=64) for o in range(PASSES)]
-        for o in range(PASSES):
-            load_words(xw_all[o], x_words[o])
+        load_words(xw_all[0], x_words[0])
 
         xs_g = keep.tile([P, S], U8, name="xs_g", align_bytes=64)
         es_g = keep.tile([P, 2, U], U8, name="es_g", tag="es_g_then_hs", align_bytes=64)
@@ -70,6 +69,7 @@ def tile_picked_yhard_hinge_p_kernel(tc, x_words, x_scales, w1, e_words, e_scale
                 out=planes[32 * q : 32 * q + 4, 0:2, :].rearrange("p a n -> p (a n)").bitcast(I32),
                 in_=xs_g[32 * q : 32 * q + 32 : 4, :].bitcast(I32),
             )
+        load_words(xw_all[1], x_words[1])
         ew_all = keep.tile([P, T], I32, name="ew_all", tag="xs_then_e", align_bytes=64)
         load_words(ew_all, e_words[0])
         nc.vector.tensor_copy(es_g[:, 0, :], es_all[:].indirect(neg_t[:]))
@@ -117,45 +117,44 @@ def tile_picked_yhard_hinge_p_kernel(tc, x_words, x_scales, w1, e_words, e_scale
                 stop=True,
             )
 
-        h_bf = []
-        for i in range(TILES):
-            tok = slice(TOK * i, TOK * (i + 1))
-            h_acc = psum.tile([P, PACK, TOK], F32, name="h_acc", tag="bank")
-            for t in range(PACK):
-                ch = slice(P * t, P * (t + 1))
-                for o in range(PASSES):
+        h_acc = [psum.tile([P, PACK, TOK], F32, name="h_acc%d" % i, tag="bank") for i in range(TILES)]
+        for o in range(PASSES):
+            for i in range(TILES):
+                tok = slice(TOK * i, TOK * (i + 1))
+                for t in range(PACK):
+                    ch = slice(P * t, P * (t + 1))
                     nc.tensor.matmul_mx(
-                        out=h_acc[:, t, :],
+                        out=h_acc[i][:, t, :],
                         lhsT=w_q[o][:, ch].bitcast(FP8X4),
                         lhsT_scale=w_s[o][:, ch],
                         rhs=xw_g[o][:, tok].bitcast(FP8X4),
                         rhs_scale=planes[:, o, tok],
-                        start=(o == 0),
-                        stop=(o == PASSES - 1),
+                        start=(o == 0 and t == 0),
+                        stop=(o == PASSES - 1 and t == PACK - 1),
                     )
-            hb = keep.tile([P, TOK, PACK], BF16, name="h_bf%d" % i, tag="h_bf%d" % i, align_bytes=64)
-            nc.scalar.copy(out=hb[:], in_=h_acc[:].rearrange("p t n -> p n t"))
-            h_bf.append(hb)
 
-        h_early = keep.tile([P, EARLY * TOK], U32, name="h_early", align_bytes=64)
-        h_q = [h_early[:, TOK * i : TOK * (i + 1)] for i in range(EARLY)]
-        h_s = keep.tile([P, S], U8, name="h_s", tag="es_g_then_hs", align_bytes=64)
+        h_bf01 = keep.tile([P, 2, TOK, PACK], BF16, name="h_bf01", tag="h_bf_then_pos", align_bytes=64)
+        h_bf23 = keep.tile([P, 2, TOK, PACK], BF16, name="h_bf23", align_bytes=64)
+        for i in range(TILES):
+            nc.scalar.copy(out=(h_bf01, h_bf23)[i // 2][:, i % 2], in_=h_acc[i][:].rearrange("p t n -> p n t"))
 
-        def quantize_h(i):
-            tok = slice(TOK * i, TOK * (i + 1))
-            nc.vector.quantize_mx(out=h_q[i].bitcast(FP8X4), scales=h_s[:, tok], in_=h_bf[i][:].rearrange("p n t -> p (n t)"))
+        h_first = keep.tile([P, TILES - 1, TOK], U32, name="h_first", align_bytes=64)
+        h_scales = keep.tile([P, TILES, TOK], U8, name="h_scales", tag="es_g_then_hs", align_bytes=64)
+        h_q = [h_first[:, i] for i in range(TILES - 1)]
+        h_s = [h_scales[:, i] for i in range(TILES)]
 
         nw_g = keep.tile([P, U], U32, name="nw_g", align_bytes=64)
         nc.vector.tensor_copy(nw_g[:], ew_all[:].bitcast(U32).indirect(neg_t[:]))
-        for i in range(EARLY):
-            quantize_h(i)
-        pw_g = keep.tile([P, U], U32, name="pw_g", tag="h_bf%d" % (EARLY - 1), align_bytes=64)
+        nc.vector.quantize_mx(
+            out=h_first[:, 0:2].rearrange("p i n -> p (i n)").bitcast(FP8X4),
+            scales=h_scales[:, 0:2].rearrange("p i n -> p (i n)"),
+            in_=h_bf01[:].rearrange("p i n t -> p (i n t)"),
+        )
+        nc.vector.quantize_mx(out=h_q[2].bitcast(FP8X4), scales=h_s[2], in_=h_bf23[:, 0].rearrange("p n t -> p (n t)"))
+        pw_g = keep.tile([P, U], U32, name="pw_g", tag="h_bf_then_pos", align_bytes=64)
         nc.vector.tensor_copy(pw_g[:], ew_all[:].bitcast(U32).indirect(pos_t[:]))
-
-        h_late = keep.tile([P, S - EARLY * TOK], U32, name="h_late", tag="xs_then_e", align_bytes=64)
-        for i in range(EARLY, TILES):
-            h_q.append(h_late[:, TOK * (i - EARLY) : TOK * (i - EARLY + 1)])
-            quantize_h(i)
+        h_last = keep.tile([P, TOK], U32, name="h_last", tag="xs_then_e", align_bytes=64)
+        h_q.append(h_last[:])
 
         sides = ((nw_g, 2, 1.0), (pw_g, 3, -1.0))
         pairs = keep.tile([P, TILES, 2, 2, V], F32, name="pairs")
@@ -165,12 +164,11 @@ def tile_picked_yhard_hinge_p_kernel(tc, x_words, x_scales, w1, e_words, e_scale
 
         def first_round(i, side):
             words, plane, sign = sides[side]
-            tok = slice(TOK * i, TOK * (i + 1))
             acc = psum.tile([P, V, D], F32, name="s_acc", tag="bank")
             nc.tensor.matmul_mx(
                 out=acc[:].rearrange("p v d -> p (v d)"),
                 lhsT=h_q[i].bitcast(FP8X4),
-                lhsT_scale=h_s[:, tok],
+                lhsT_scale=h_s[i],
                 rhs=words[:].bitcast(FP8X4),
                 rhs_scale=planes[:, plane, :],
                 start=True,
@@ -192,10 +190,12 @@ def tile_picked_yhard_hinge_p_kernel(tc, x_words, x_scales, w1, e_words, e_scale
             nc.vector.tensor_scalar(out=loss[:, i], in0=gap[:, i], scalar1=MARGIN, scalar2=0.0, op0=ALU.add, op1=ALU.max)
             nc.sync.dma_start(out=out[TOK * i : TOK * (i + 1), :], in_=loss[:, i])
 
-        for side in range(2):
-            for i in range(2):
-                first_round(i, side)
+        for i in range(2):
+            first_round(i, 0)
+        nc.vector.quantize_mx(out=h_q[3].bitcast(FP8X4), scales=h_s[3], in_=h_bf23[:, 1].rearrange("p n t -> p (n t)"))
         first_round(2, 0)
+        for i in range(2):
+            first_round(i, 1)
         second_round(0, 2)
         difference(0, 2, nc.gpsimd)
         first_round(2, 1)

@@ -56,8 +56,8 @@ def tile_picked_yhard_hinge_p_kernel(tc, x_words, x_scales, w1, e_words, e_scale
         nc.sync.dma_start(out=xs_all[0:P:4, :].bitcast(I32), in_=x_scales.rearrange("o q c -> q o c").bitcast(I32))
         nc.sync.dma_start(neg_t[:], neg)
         nc.sync.dma_start(out=es_all[0:P:8, :].bitcast(I32), in_=e_scales[0].bitcast(I32))
-        load_w(1)
         nc.sync.dma_start(pos_t[:], pos)
+        load_w(1)
         xw_all = [keep.tile([P, T], I32, name="xw_all%d" % o, tag="xw%d" % o, align_bytes=64) for o in range(PASSES)]
         load_words(xw_all[0], x_words[0])
 
@@ -105,17 +105,20 @@ def tile_picked_yhard_hinge_p_kernel(tc, x_words, x_scales, w1, e_words, e_scale
                 xw_all[1][:].bitcast(U32).indirect(offs_t[:, 16 * half : 16 * (half + 1)]),
             )
 
-        for t in range(4):
+        def warm_up(t, words, scales):
             idle = psum.tile([P, S], F32, name="idle", tag="bank")
             nc.tensor.matmul_mx(
                 out=idle[:],
                 lhsT=w_q[0][:, P * t : P * (t + 1)].bitcast(FP8X4),
                 lhsT_scale=w_s[0][:, P * t : P * (t + 1)],
-                rhs=w_q[0][:].bitcast(FP8X4),
-                rhs_scale=w_s[0][:],
+                rhs=words.bitcast(FP8X4),
+                rhs_scale=scales,
                 start=True,
                 stop=True,
             )
+
+        for t in range(2):
+            warm_up(t, w_q[0][:], w_s[0][:])
 
         h_acc = [psum.tile([P, PACK, TOK], F32, name="h_acc%d" % i, tag="bank") for i in range(TILES)]
         for o in range(PASSES):
@@ -133,28 +136,30 @@ def tile_picked_yhard_hinge_p_kernel(tc, x_words, x_scales, w1, e_words, e_scale
                         stop=(o == PASSES - 1 and t == PACK - 1),
                     )
 
+        for t in range(2):
+            warm_up(t, xw_g[0][:], planes[:, 2, :])
+
         h_bf01 = keep.tile([P, 2, TOK, PACK], BF16, name="h_bf01", tag="h_bf_then_pos", align_bytes=64)
         h_bf23 = keep.tile([P, 2, TOK, PACK], BF16, name="h_bf23", align_bytes=64)
-        for i in range(TILES):
+        nc.vector.tensor_copy(out=h_bf01[:, 0], in_=h_acc[0][:].rearrange("p t n -> p n t"))
+        for i in range(1, TILES):
             nc.scalar.copy(out=(h_bf01, h_bf23)[i // 2][:, i % 2], in_=h_acc[i][:].rearrange("p t n -> p n t"))
 
-        h_first = keep.tile([P, TILES - 1, TOK], U32, name="h_first", align_bytes=64)
+        h_codes = keep.tile([P, TILES, TOK], U32, name="h_codes", align_bytes=64)
         h_scales = keep.tile([P, TILES, TOK], U8, name="h_scales", tag="es_g_then_hs", align_bytes=64)
-        h_q = [h_first[:, i] for i in range(TILES - 1)]
+        h_q = [h_codes[:, i] for i in range(TILES)]
         h_s = [h_scales[:, i] for i in range(TILES)]
 
         nw_g = keep.tile([P, U], U32, name="nw_g", align_bytes=64)
         nc.vector.tensor_copy(nw_g[:], ew_all[:].bitcast(U32).indirect(neg_t[:]))
-        nc.vector.quantize_mx(
-            out=h_first[:, 0:2].rearrange("p i n -> p (i n)").bitcast(FP8X4),
-            scales=h_scales[:, 0:2].rearrange("p i n -> p (i n)"),
-            in_=h_bf01[:].rearrange("p i n t -> p (i n t)"),
-        )
-        nc.vector.quantize_mx(out=h_q[2].bitcast(FP8X4), scales=h_s[2], in_=h_bf23[:, 0].rearrange("p n t -> p (n t)"))
+        for g, values in enumerate((h_bf01, h_bf23)):
+            nc.vector.quantize_mx(
+                out=h_codes[:, 2 * g : 2 * g + 2].rearrange("p i n -> p (i n)").bitcast(FP8X4),
+                scales=h_scales[:, 2 * g : 2 * g + 2].rearrange("p i n -> p (i n)"),
+                in_=values[:].rearrange("p i n t -> p (i n t)"),
+            )
         pw_g = keep.tile([P, U], U32, name="pw_g", tag="h_bf_then_pos", align_bytes=64)
         nc.vector.tensor_copy(pw_g[:], ew_all[:].bitcast(U32).indirect(pos_t[:]))
-        h_last = keep.tile([P, TOK], U32, name="h_last", tag="xs_then_e", align_bytes=64)
-        h_q.append(h_last[:])
 
         sides = ((nw_g, 2, 1.0), (pw_g, 3, -1.0))
         pairs = keep.tile([P, TILES, 2, 2, V], F32, name="pairs")
@@ -183,6 +188,9 @@ def tile_picked_yhard_hinge_p_kernel(tc, x_words, x_scales, w1, e_words, e_scale
             both = pairs[:, lo:hi].rearrange("p i s d v -> p (i s) d v")
             nc.vector.tensor_tensor(out=best[:, lo:hi].rearrange("p i s v -> p (i s) v"), in0=both[:, :, 0], in1=both[:, :, 1], op=ALU.max)
 
+        def second_round_of_side(lo, hi, side):
+            nc.vector.tensor_tensor(out=best[:, lo:hi, side], in0=pairs[:, lo:hi, side, 0], in1=pairs[:, lo:hi, side, 1], op=ALU.max)
+
         def difference(lo, hi, engine):
             engine.tensor_tensor(out=gap[:, lo:hi], in0=best[:, lo:hi, 0], in1=best[:, lo:hi, 1], op=ALU.add)
 
@@ -190,13 +198,13 @@ def tile_picked_yhard_hinge_p_kernel(tc, x_words, x_scales, w1, e_words, e_scale
             nc.vector.tensor_scalar(out=loss[:, i], in0=gap[:, i], scalar1=MARGIN, scalar2=0.0, op0=ALU.add, op1=ALU.max)
             nc.sync.dma_start(out=out[TOK * i : TOK * (i + 1), :], in_=loss[:, i])
 
-        for i in range(2):
+        for i in range(3):
             first_round(i, 0)
-        nc.vector.quantize_mx(out=h_q[3].bitcast(FP8X4), scales=h_s[3], in_=h_bf23[:, 1].rearrange("p n t -> p (n t)"))
-        first_round(2, 0)
+        second_round_of_side(0, 2, 0)
         for i in range(2):
             first_round(i, 1)
-        second_round(0, 2)
+        second_round_of_side(2, 3, 0)
+        second_round_of_side(0, 2, 1)
         difference(0, 2, nc.gpsimd)
         first_round(2, 1)
         first_round(3, 0)
@@ -204,7 +212,7 @@ def tile_picked_yhard_hinge_p_kernel(tc, x_words, x_scales, w1, e_words, e_scale
         early = keep.tile([P, 2, V], F32, name="early", tag="upper3_0")
         nc.scalar.activation(out=early[:], in_=gap[:, 0:2], func=ACT.Relu, bias=MARGIN)
         nc.sync.dma_start(out=out[0 : 2 * TOK, :].rearrange("(i p) v -> p i v", p=TOK), in_=early[:])
-        second_round(2, 3)
+        second_round_of_side(2, 3, 1)
         second_round(3, 4)
         difference(2, 3, nc.vector)
         difference(3, 4, nc.vector)

@@ -161,14 +161,14 @@ def tile_picked_yhard_hinge_p_kernel(tc, x_words, x_scales, w1, e_words, e_scale
         pw_g = keep.tile([P, U], U32, name="pw_g", tag="h_bf_then_pos", align_bytes=64)
         nc.vector.tensor_copy(pw_g[:], ew_all[:].bitcast(U32).indirect(pos_t[:]))
 
-        sides = ((nw_g, 2, 1.0), (pw_g, 3, -1.0))
+        sides = ((nw_g, 2), (pw_g, 3))
         pairs = keep.tile([P, TILES, 2, 2, V], F32, name="pairs")
         best = keep.tile([P, TILES, 2, V], F32, name="best")
         gap = keep.tile([P, TILES, V], F32, name="gap")
         loss = keep.tile([P, TILES, V], F32, name="loss")
 
         def first_round(i, side):
-            words, plane, sign = sides[side]
+            words, plane = sides[side]
             acc = psum.tile([P, V, D], F32, name="s_acc", tag="bank")
             nc.tensor.matmul_mx(
                 out=acc[:].rearrange("p v d -> p (v d)"),
@@ -181,12 +181,12 @@ def tile_picked_yhard_hinge_p_kernel(tc, x_words, x_scales, w1, e_words, e_scale
             )
             by_entry = acc[:].rearrange("p v d -> p d v")
             upper = keep.tile([P, 2, V], F32, name="upper%d_%d" % (i, side), tag="upper%d_%d" % (i, side))
-            nc.scalar.activation(out=upper[:], in_=by_entry[:, 2:4], func=ACT.Copy, scale=sign)
-            nc.vector.scalar_tensor_tensor(out=pairs[:, i, side], in0=by_entry[:, 0:2], scalar=sign, in1=upper[:], op0=ALU.mult, op1=ALU.max)
-
-        def second_round(lo, hi):
-            both = pairs[:, lo:hi].rearrange("p i s d v -> p (i s) d v")
-            nc.vector.tensor_tensor(out=best[:, lo:hi].rearrange("p i s v -> p (i s) v"), in0=both[:, :, 0], in1=both[:, :, 1], op=ALU.max)
+            if side == 0:
+                nc.scalar.activation(out=upper[:], in_=by_entry[:, 2:4], func=ACT.Copy, bias=MARGIN)
+                nc.vector.scalar_tensor_tensor(out=pairs[:, i, side], in0=by_entry[:, 0:2], scalar=MARGIN, in1=upper[:], op0=ALU.add, op1=ALU.max)
+            else:
+                nc.scalar.activation(out=upper[:], in_=by_entry[:, 2:4], func=ACT.Copy, scale=-1.0)
+                nc.vector.scalar_tensor_tensor(out=pairs[:, i, side], in0=by_entry[:, 0:2], scalar=-1.0, in1=upper[:], op0=ALU.mult, op1=ALU.max)
 
         def second_round_of_side(lo, hi, side):
             nc.vector.tensor_tensor(out=best[:, lo:hi, side], in0=pairs[:, lo:hi, side, 0], in1=pairs[:, lo:hi, side, 1], op=ALU.max)
@@ -194,27 +194,26 @@ def tile_picked_yhard_hinge_p_kernel(tc, x_words, x_scales, w1, e_words, e_scale
         def difference(lo, hi, engine):
             engine.tensor_tensor(out=gap[:, lo:hi], in0=best[:, lo:hi, 0], in1=best[:, lo:hi, 1], op=ALU.add)
 
-        def hinge_on_vector(i):
-            nc.vector.tensor_scalar(out=loss[:, i], in0=gap[:, i], scalar1=MARGIN, scalar2=0.0, op0=ALU.add, op1=ALU.max)
-            nc.sync.dma_start(out=out[TOK * i : TOK * (i + 1), :], in_=loss[:, i])
-
         for i in range(3):
             first_round(i, 0)
         second_round_of_side(0, 2, 0)
+        second_round_of_side(2, 3, 0)
         for i in range(2):
             first_round(i, 1)
-        second_round_of_side(2, 3, 0)
-        second_round_of_side(0, 2, 1)
-        difference(0, 2, nc.gpsimd)
+        for i in range(2):
+            second_round_of_side(i, i + 1, 1)
+            difference(i, i + 1, nc.gpsimd)
         first_round(2, 1)
         first_round(3, 0)
         first_round(3, 1)
-        early = keep.tile([P, 2, V], F32, name="early", tag="upper3_0")
-        nc.scalar.activation(out=early[:], in_=gap[:, 0:2], func=ACT.Relu, bias=MARGIN)
-        nc.sync.dma_start(out=out[0 : 2 * TOK, :].rearrange("(i p) v -> p i v", p=TOK), in_=early[:])
-        second_round_of_side(2, 3, 1)
-        second_round(3, 4)
-        difference(2, 3, nc.vector)
-        difference(3, 4, nc.vector)
-        hinge_on_vector(2)
-        hinge_on_vector(3)
+        for i, tag in ((0, "upper2_1"), (1, "upper3_0")):
+            early = keep.tile([P, V], F32, name="early%d" % i, tag=tag)
+            nc.scalar.activation(out=early[:], in_=gap[:, i], func=ACT.Relu)
+            nc.sync.dma_start(out=out[TOK * i : TOK * (i + 1), :], in_=early[:])
+        second_round_of_side(3, 4, 0)
+        sums = keep.tile([P, 2, 2, V], F32, name="sums")
+        for i in (2, 3):
+            nc.vector.tensor_tensor(out=sums[:, i - 2], in0=pairs[:, i, 1], in1=best[:, i, 0:1].to_broadcast([P, 2, V]), op=ALU.add)
+        for i in (2, 3):
+            nc.vector.scalar_tensor_tensor(out=loss[:, i], in0=sums[:, i - 2, 0], scalar=0.0, in1=sums[:, i - 2, 1], op0=ALU.max, op1=ALU.max)
+            nc.sync.dma_start(out=out[TOK * i : TOK * (i + 1), :], in_=loss[:, i])

@@ -194,23 +194,22 @@ def tile_picked_yhard_hinge_p_kernel(tc, x_words, x_scales, w1, e_words, e_scale
         def difference(lo, hi, engine):
             engine.tensor_tensor(out=gap[:, lo:hi], in0=best[:, lo:hi, 0], in1=best[:, lo:hi, 1], op=ALU.add)
 
-        for i in range(3):
+        for i in range(TILES):
             first_round(i, 0)
         second_round_of_side(0, 2, 0)
-        second_round_of_side(2, 3, 0)
         for i in range(2):
             first_round(i, 1)
-        for i in range(2):
-            second_round_of_side(i, i + 1, 1)
-            difference(i, i + 1, nc.gpsimd)
+        second_round_of_side(0, 1, 1)
+        difference(0, 1, nc.gpsimd)
+        second_round_of_side(2, 4, 0)
+        second_round_of_side(1, 2, 1)
+        difference(1, 2, nc.gpsimd)
         first_round(2, 1)
-        first_round(3, 0)
         first_round(3, 1)
-        for i, tag in ((0, "upper2_1"), (1, "upper3_0")):
+        for i, tag in ((0, "upper2_1"), (1, "upper3_1")):
             early = keep.tile([P, V], F32, name="early%d" % i, tag=tag)
             nc.scalar.activation(out=early[:], in_=gap[:, i], func=ACT.Relu)
             nc.sync.dma_start(out=out[TOK * i : TOK * (i + 1), :], in_=early[:])
-        second_round_of_side(3, 4, 0)
         sums = keep.tile([P, 2, 2, V], F32, name="sums")
         for i in (2, 3):
             nc.vector.tensor_tensor(out=sums[:, i - 2], in0=pairs[:, i, 1], in1=best[:, i, 0:1].to_broadcast([P, 2, V]), op=ALU.add)

@@ -30,20 +30,21 @@ def tile_picked_yhard_hinge_p_kernel(tc, x_words, x_scales, w1, e_words, e_scale
     with ExitStack() as ctx:
         lists = ctx.enter_context(tc.tile_pool(name="lists", bufs=1))
         keep = ctx.enter_context(tc.tile_pool(name="keep", bufs=1))
+        shared = ctx.enter_context(tc.tile_pool(name="shared", bufs=1))
         psum = ctx.enter_context(tc.psum_pool(name="psum", bufs=8))
 
         offs_t = lists.tile([P, S // 16], U16, name="offs_t")
         neg_t = lists.tile([P, U // 16], U16, name="neg_t")
         pos_t = lists.tile([P, U // 16], U16, name="pos_t")
 
-        xs_all = keep.tile([P, T], U8, name="xs_all", tag="xs_then_e", align_bytes=64)
+        xs_all = keep.tile([P, T], U8, name="xs_all", align_bytes=64)
         es_all = keep.tile([P, T], U8, name="es_all", align_bytes=64)
-        planes = keep.tile([P, 4, S], U8, name="planes", align_bytes=64)
+        planes = keep.tile([P, 2, S], U8, name="planes", align_bytes=64)
         nc.vector.memset(xs_all[:].bitcast(I32), 0)
         nc.vector.memset(es_all[:].bitcast(I32), 0)
         nc.vector.memset(planes[:].rearrange("p a n -> p (a n)").bitcast(I32), 0)
 
-        w_raw = [keep.tile([P, PACK, H], F32, name="w_raw%d" % o) for o in range(PASSES)]
+        w_raw = [shared.tile([P, PACK, H], F32, name="w_raw0", offset=4096, align_bytes=64), keep.tile([P, PACK, H], F32, name="w_raw1")]
 
         def load_w(o):
             nc.sync.dma_start(out=w_raw[o][:], in_=w1[512 * o : 512 * (o + 1), :].rearrange("(p j) c -> p j c", j=PACK))
@@ -58,37 +59,44 @@ def tile_picked_yhard_hinge_p_kernel(tc, x_words, x_scales, w1, e_words, e_scale
         nc.sync.dma_start(out=es_all[0:P:8, :].bitcast(I32), in_=e_scales[0].bitcast(I32))
         nc.sync.dma_start(pos_t[:], pos)
         load_w(1)
-        xw_all = [keep.tile([P, T], I32, name="xw_all%d" % o, tag="xw%d" % o, align_bytes=64) for o in range(PASSES)]
+        xw_all = [keep.tile([P, T], I32, name="xw_all0", tag="xw0", align_bytes=64)]
         load_words(xw_all[0], x_words[0])
 
         xs_g = keep.tile([P, S], U8, name="xs_g", align_bytes=64)
         es_g = keep.tile([P, 2, U], U8, name="es_g", tag="es_g_then_hs", align_bytes=64)
         nc.vector.tensor_copy(xs_g[:], xs_all[:].indirect(offs_t[:]))
-        for q in range(4):
-            nc.sync.dma_start(
-                out=planes[32 * q : 32 * q + 4, 0:2, :].rearrange("p a n -> p (a n)").bitcast(I32),
-                in_=xs_g[32 * q : 32 * q + 32 : 4, :].bitcast(I32),
-            )
-        load_words(xw_all[1], x_words[1])
-        ew_all = keep.tile([P, T], I32, name="ew_all", tag="xs_then_e", align_bytes=64)
-        load_words(ew_all, e_words[0])
-        nc.vector.tensor_copy(es_g[:, 0, :], es_all[:].indirect(neg_t[:]))
-        nc.vector.tensor_copy(es_g[:, 1, :], es_all[:].indirect(pos_t[:]))
-        for q in range(4):
-            nc.sync.dma_start(
-                out=planes[32 * q : 32 * q + 4, 2:4, :].rearrange("p a n -> p (a n)").bitcast(I32),
-                in_=es_g[32 * q : 32 * q + 32 : 8, :, :].rearrange("p a n -> p (a n)").bitcast(I32),
-            )
-
         w_bf = [keep.tile([P, PACK, P, PACK], BF16, name="w_bf%d" % o, align_bytes=64) for o in range(PASSES)]
-        w_q = []
-        w_s = []
-        for o in range(PASSES):
+
+        def cast_w(o):
             nc.scalar.activation(
                 out=w_bf[o][:].rearrange("p t m j -> p m t j"),
                 in_=w_raw[o][:].rearrange("p j (m t) -> p m t j", t=PACK),
                 func=ACT.Copy,
             )
+
+        cast_w(0)
+        for q in range(4):
+            nc.scalar.dma_start(
+                out=planes[32 * q : 32 * q + 4].rearrange("p a n -> p (a n)").bitcast(I32),
+                in_=xs_g[32 * q : 32 * q + 32 : 4, :].bitcast(I32),
+            )
+        xw_all.append(shared.tile([P, T], I32, name="xw_all1", offset=0, align_bytes=64))
+        load_words(xw_all[1], x_words[1])
+        ew_all = shared.tile([P, T], I32, name="ew_all", offset=9216, align_bytes=64)
+        e_planes = shared.tile([P, 2, U], U8, name="e_planes", offset=8192, align_bytes=64)
+        nc.gpsimd.memset(e_planes[:].rearrange("p a n -> p (a n)").bitcast(I32), 0)
+        load_words(ew_all, e_words[0])
+        nc.vector.tensor_copy(es_g[:, 0, :], es_all[:].indirect(neg_t[:]))
+        nc.vector.tensor_copy(es_g[:, 1, :], es_all[:].indirect(pos_t[:]))
+        for q in range(4):
+            nc.sync.dma_start(
+                out=e_planes[32 * q : 32 * q + 4].rearrange("p a n -> p (a n)").bitcast(I32),
+                in_=es_g[32 * q : 32 * q + 32 : 8, :, :].rearrange("p a n -> p (a n)").bitcast(I32),
+            )
+
+        w_q = []
+        w_s = []
+        cast_w(1)
 
         def quantize_w(o, codes_tag, scales_tag):
             w_q.append(keep.tile([P, H], U32, name="w_q%d" % o, tag=codes_tag, align_bytes=64))
@@ -137,7 +145,7 @@ def tile_picked_yhard_hinge_p_kernel(tc, x_words, x_scales, w1, e_words, e_scale
                     )
 
         for t in range(2):
-            warm_up(t, xw_g[0][:], planes[:, 2, :])
+            warm_up(t, xw_g[0][:], e_planes[:, 0, :])
 
         h_bf01 = keep.tile([P, 2, TOK, PACK], BF16, name="h_bf01", tag="h_bf_then_pos", align_bytes=64)
         h_bf23 = keep.tile([P, 2, TOK, PACK], BF16, name="h_bf23", align_bytes=64)
@@ -161,7 +169,7 @@ def tile_picked_yhard_hinge_p_kernel(tc, x_words, x_scales, w1, e_words, e_scale
         pw_g = keep.tile([P, U], U32, name="pw_g", tag="h_bf_then_pos", align_bytes=64)
         nc.vector.tensor_copy(pw_g[:], ew_all[:].bitcast(U32).indirect(pos_t[:]))
 
-        sides = ((nw_g, 2), (pw_g, 3))
+        sides = ((nw_g, 0), (pw_g, 1))
         pairs = keep.tile([P, TILES, 2, 2, V], F32, name="pairs")
         best = keep.tile([P, TILES, 2, V], F32, name="best")
         gap = keep.tile([P, TILES, V], F32, name="gap")
@@ -175,7 +183,7 @@ def tile_picked_yhard_hinge_p_kernel(tc, x_words, x_scales, w1, e_words, e_scale
                 lhsT=h_q[i].bitcast(FP8X4),
                 lhsT_scale=h_s[i],
                 rhs=words[:].bitcast(FP8X4),
-                rhs_scale=planes[:, plane, :],
+                rhs_scale=e_planes[:, plane, :],
                 start=True,
                 stop=True,
             )

@@ -63,9 +63,9 @@ def tile_picked_yhard_hinge_p_kernel(tc, x_words, x_scales, w1, e_words, e_scale
         load_words(xw_all[0], x_words[0])
 
         xs_g = keep.tile([P, S], U8, name="xs_g", align_bytes=64)
-        es_g = keep.tile([P, 2, U], U8, name="es_g", tag="es_g_then_hs", align_bytes=64)
+        es_g = keep.tile([P, 2, U], U8, name="es_g", align_bytes=64)
         nc.vector.tensor_copy(xs_g[:], xs_all[:].indirect(offs_t[:]))
-        w_bf = [keep.tile([P, PACK, P, PACK], BF16, name="w_bf%d" % o, align_bytes=64) for o in range(PASSES)]
+        w_bf = [keep.tile([P, PACK, P, PACK], BF16, name="w_bf%d" % o, tag="w_bf%d" % o, align_bytes=64) for o in range(PASSES)]
 
         def cast_w(o):
             nc.scalar.activation(
@@ -88,11 +88,6 @@ def tile_picked_yhard_hinge_p_kernel(tc, x_words, x_scales, w1, e_words, e_scale
         load_words(ew_all, e_words[0])
         nc.vector.tensor_copy(es_g[:, 0, :], es_all[:].indirect(neg_t[:]))
         nc.vector.tensor_copy(es_g[:, 1, :], es_all[:].indirect(pos_t[:]))
-        for q in range(4):
-            nc.sync.dma_start(
-                out=e_planes[32 * q : 32 * q + 4].rearrange("p a n -> p (a n)").bitcast(I32),
-                in_=es_g[32 * q : 32 * q + 32 : 8, :, :].rearrange("p a n -> p (a n)").bitcast(I32),
-            )
 
         w_q = []
         w_s = []
@@ -104,6 +99,13 @@ def tile_picked_yhard_hinge_p_kernel(tc, x_words, x_scales, w1, e_words, e_scale
             nc.vector.quantize_mx(out=w_q[o][:].bitcast(FP8X4), scales=w_s[o][:], in_=w_bf[o][:].rearrange("p t m j -> p (t m j)"))
 
         quantize_w(0, "wq0", "ws0")
+        es_m = keep.tile([P, 2, U], U8, name="es_m", tag="w_bf0", align_bytes=64)
+        nc.vector.tensor_copy(es_m[:].rearrange("p a (d v) -> p a d v", d=D), es_g[:].rearrange("p a (v d) -> p a d v", d=D))
+        for q in range(4):
+            nc.sync.dma_start(
+                out=e_planes[32 * q : 32 * q + 4].rearrange("p a n -> p (a n)").bitcast(I32),
+                in_=es_m[32 * q : 32 * q + 32 : 8, :, :].rearrange("p a n -> p (a n)").bitcast(I32),
+            )
         xw_g = [keep.tile([P, S], U32, name="xw_g%d" % o, align_bytes=64) for o in range(PASSES)]
         nc.vector.tensor_copy(xw_g[0][:], xw_all[0][:].bitcast(U32).indirect(offs_t[:]))
         quantize_w(1, "xw0", "ws1")
@@ -154,12 +156,12 @@ def tile_picked_yhard_hinge_p_kernel(tc, x_words, x_scales, w1, e_words, e_scale
             nc.scalar.copy(out=(h_bf01, h_bf23)[i // 2][:, i % 2], in_=h_acc[i][:].rearrange("p t n -> p n t"))
 
         h_codes = keep.tile([P, TILES, TOK], U32, name="h_codes", align_bytes=64)
-        h_scales = keep.tile([P, TILES, TOK], U8, name="h_scales", tag="es_g_then_hs", align_bytes=64)
+        h_scales = keep.tile([P, TILES, TOK], U8, name="h_scales", tag="w_bf0", align_bytes=64)
         h_q = [h_codes[:, i] for i in range(TILES)]
         h_s = [h_scales[:, i] for i in range(TILES)]
 
         nw_g = keep.tile([P, U], U32, name="nw_g", align_bytes=64)
-        nc.vector.tensor_copy(nw_g[:], ew_all[:].bitcast(U32).indirect(neg_t[:]))
+        nc.vector.tensor_copy(nw_g[:].rearrange("p (d v) -> p v d", d=D), ew_all[:].bitcast(U32).indirect(neg_t[:]))
         for g, values in enumerate((h_bf01, h_bf23)):
             nc.vector.quantize_mx(
                 out=h_codes[:, 2 * g : 2 * g + 2].rearrange("p i n -> p (i n)").bitcast(FP8X4),
@@ -167,7 +169,7 @@ def tile_picked_yhard_hinge_p_kernel(tc, x_words, x_scales, w1, e_words, e_scale
                 in_=values[:].rearrange("p i n t -> p (i n t)"),
             )
         pw_g = keep.tile([P, U], U32, name="pw_g", tag="h_bf_then_pos", align_bytes=64)
-        nc.vector.tensor_copy(pw_g[:], ew_all[:].bitcast(U32).indirect(pos_t[:]))
+        nc.vector.tensor_copy(pw_g[:].rearrange("p (d v) -> p v d", d=D), ew_all[:].bitcast(U32).indirect(pos_t[:]))
 
         sides = ((nw_g, 0), (pw_g, 1))
         pairs = keep.tile([P, TILES, 2, 2, V], F32, name="pairs")
@@ -177,9 +179,9 @@ def tile_picked_yhard_hinge_p_kernel(tc, x_words, x_scales, w1, e_words, e_scale
 
         def first_round(i, side):
             words, plane = sides[side]
-            acc = psum.tile([P, V, D], F32, name="s_acc", tag="bank")
+            acc = psum.tile([P, D, V], F32, name="s_acc", tag="bank")
             nc.tensor.matmul_mx(
-                out=acc[:].rearrange("p v d -> p (v d)"),
+                out=acc[:].rearrange("p d v -> p (d v)"),
                 lhsT=h_q[i].bitcast(FP8X4),
                 lhsT_scale=h_s[i],
                 rhs=words[:].bitcast(FP8X4),
@@ -187,7 +189,7 @@ def tile_picked_yhard_hinge_p_kernel(tc, x_words, x_scales, w1, e_words, e_scale
                 start=True,
                 stop=True,
             )
-            by_entry = acc[:].rearrange("p v d -> p d v")
+            by_entry = acc[:]
             upper = keep.tile([P, 2, V], F32, name="upper%d_%d" % (i, side), tag="upper%d_%d" % (i, side))
             if side == 0:
                 nc.scalar.activation(out=upper[:], in_=by_entry[:, 2:4], func=ACT.Copy, bias=MARGIN)

@@ -65,7 +65,7 @@ def tile_picked_yhard_hinge_p_kernel(tc, x_words, x_scales, w1, e_words, e_scale
         xs_g = keep.tile([P, S], U8, name="xs_g", align_bytes=64)
         es_g = keep.tile([P, 2, U], U8, name="es_g", align_bytes=64)
         nc.vector.tensor_copy(xs_g[:], xs_all[:].indirect(offs_t[:]))
-        w_bf = [keep.tile([P, PACK, P, PACK], BF16, name="w_bf%d" % o, tag="w_bf%d" % o, align_bytes=64) for o in range(PASSES)]
+        w_bf = [keep.tile([P, PACK, P, PACK], BF16, name="w_bf%d" % o, align_bytes=64) for o in range(PASSES)]
 
         def cast_w(o):
             nc.scalar.activation(
@@ -82,7 +82,7 @@ def tile_picked_yhard_hinge_p_kernel(tc, x_words, x_scales, w1, e_words, e_scale
             )
         xw_all.append(shared.tile([P, T], I32, name="xw_all1", offset=0, align_bytes=64))
         load_words(xw_all[1], x_words[1])
-        ew_all = shared.tile([P, T], I32, name="ew_all", offset=9216, align_bytes=64)
+        ew_all = shared.tile([P, T], I32, name="ew_all", offset=10240, align_bytes=64)
         e_planes = shared.tile([P, 2, U], U8, name="e_planes", offset=8192, align_bytes=64)
         nc.gpsimd.memset(e_planes[:].rearrange("p a n -> p (a n)").bitcast(I32), 0)
         load_words(ew_all, e_words[0])
@@ -99,7 +99,7 @@ def tile_picked_yhard_hinge_p_kernel(tc, x_words, x_scales, w1, e_words, e_scale
             nc.vector.quantize_mx(out=w_q[o][:].bitcast(FP8X4), scales=w_s[o][:], in_=w_bf[o][:].rearrange("p t m j -> p (t m j)"))
 
         quantize_w(0, "wq0", "ws0")
-        es_m = keep.tile([P, 2, U], U8, name="es_m", tag="w_bf0", align_bytes=64)
+        es_m = shared.tile([P, 2, U], U8, name="es_m", offset=9216, align_bytes=64)
         nc.vector.tensor_copy(es_m[:].rearrange("p a (d v) -> p a d v", d=D), es_g[:].rearrange("p a (v d) -> p a d v", d=D))
         for q in range(4):
             nc.sync.dma_start(
@@ -108,7 +108,7 @@ def tile_picked_yhard_hinge_p_kernel(tc, x_words, x_scales, w1, e_words, e_scale
             )
         xw_g = [keep.tile([P, S], U32, name="xw_g%d" % o, align_bytes=64) for o in range(PASSES)]
         nc.vector.tensor_copy(xw_g[0][:], xw_all[0][:].bitcast(U32).indirect(offs_t[:]))
-        quantize_w(1, "xw0", "ws1")
+        quantize_w(1, "wq1", "ws1")
         for half in range(2):
             nc.vector.tensor_copy(
                 xw_g[1][:, 256 * half : 256 * (half + 1)],
@@ -156,7 +156,7 @@ def tile_picked_yhard_hinge_p_kernel(tc, x_words, x_scales, w1, e_words, e_scale
             nc.scalar.copy(out=(h_bf01, h_bf23)[i // 2][:, i % 2], in_=h_acc[i][:].rearrange("p t n -> p n t"))
 
         h_codes = keep.tile([P, TILES, TOK], U32, name="h_codes", align_bytes=64)
-        h_scales = keep.tile([P, TILES, TOK], U8, name="h_scales", tag="w_bf0", align_bytes=64)
+        h_scales = shared.tile([P, TILES, TOK], U8, name="h_scales", offset=9216, align_bytes=64)
         h_q = [h_codes[:, i] for i in range(TILES)]
         h_s = [h_scales[:, i] for i in range(TILES)]
 

@@ -1,6 +1,7 @@
 from contextlib import ExitStack
 
 import concourse.mybir as mybir
+from concourse.masks import make_identity
 
 K, T, S, H, D, U = 1024, 2048, 512, 512, 4, 512
 FLOPS = 2 * K * H * S + 2 * 2 * H * S * U
@@ -22,7 +23,7 @@ TOK = 128
 TILES = S // TOK
 V = U // D
 MARGIN = 0.3
-EARLY = 2
+TURNED = 2
 
 
 def tile_picked_yhard_hinge_p_kernel(tc, x_words, x_scales, w1, e_words, e_scales, offs, pos, neg, out):
@@ -43,6 +44,9 @@ def tile_picked_yhard_hinge_p_kernel(tc, x_words, x_scales, w1, e_words, e_scale
         nc.vector.memset(xs_all[:].bitcast(I32), 0)
         nc.vector.memset(es_all[:].bitcast(I32), 0)
         nc.vector.memset(planes[:].rearrange("p a n -> p (a n)").bitcast(I32), 0)
+
+        identity = keep.tile([P, P], F32, name="identity")
+        make_identity(nc, identity[:])
 
         w_raw = [shared.tile([P, PACK, H], F32, name="w_raw0", offset=4096, align_bytes=64), keep.tile([P, PACK, H], F32, name="w_raw1")]
 
@@ -171,58 +175,84 @@ def tile_picked_yhard_hinge_p_kernel(tc, x_words, x_scales, w1, e_words, e_scale
         pw_g = keep.tile([P, U], U32, name="pw_g", tag="h_bf_then_pos", align_bytes=64)
         nc.vector.tensor_copy(pw_g[:].rearrange("p (d v) -> p v d", d=D), ew_all[:].bitcast(U32).indirect(pos_t[:]))
 
+        def scores(lhsT, lhsT_scale, rhs, rhs_scale, acc):
+            nc.tensor.matmul_mx(
+                out=acc,
+                lhsT=lhsT.bitcast(FP8X4),
+                lhsT_scale=lhsT_scale,
+                rhs=rhs.bitcast(FP8X4),
+                rhs_scale=rhs_scale,
+                start=True,
+                stop=True,
+            )
+
+        def add_turned(acc, values, start, stop):
+            nc.tensor.matmul(acc, lhsT=values, rhs=identity[:], is_transpose=True, start=start, stop=stop)
+
         sides = ((nw_g, 0), (pw_g, 1))
         pairs = keep.tile([P, TILES, 2, 2, V], F32, name="pairs")
-        best = keep.tile([P, TILES, 2, V], F32, name="best")
-        gap = keep.tile([P, TILES, V], F32, name="gap")
-        loss = keep.tile([P, TILES, V], F32, name="loss")
+        best = keep.tile([P, TILES, V], F32, name="best")
 
         def first_round(i, side):
             words, plane = sides[side]
             acc = psum.tile([P, D, V], F32, name="s_acc", tag="bank")
-            nc.tensor.matmul_mx(
-                out=acc[:].rearrange("p d v -> p (d v)"),
-                lhsT=h_q[i].bitcast(FP8X4),
-                lhsT_scale=h_s[i],
-                rhs=words[:].bitcast(FP8X4),
-                rhs_scale=e_planes[:, plane, :],
-                start=True,
-                stop=True,
-            )
-            by_entry = acc[:]
-            upper = keep.tile([P, 2, V], F32, name="upper%d_%d" % (i, side), tag="upper%d_%d" % (i, side))
-            if side == 0:
-                nc.scalar.activation(out=upper[:], in_=by_entry[:, 2:4], func=ACT.Copy, bias=MARGIN)
-                nc.vector.scalar_tensor_tensor(out=pairs[:, i, side], in0=by_entry[:, 0:2], scalar=MARGIN, in1=upper[:], op0=ALU.add, op1=ALU.max)
+            if i < TURNED:
+                for d in range(D):
+                    cols = slice(V * d, V * (d + 1))
+                    scores(words[:, cols], e_planes[:, plane, cols], h_q[i], h_s[i], acc[:, d])
             else:
-                nc.scalar.activation(out=upper[:], in_=by_entry[:, 2:4], func=ACT.Copy, scale=-1.0)
-                nc.vector.scalar_tensor_tensor(out=pairs[:, i, side], in0=by_entry[:, 0:2], scalar=-1.0, in1=upper[:], op0=ALU.mult, op1=ALU.max)
+                scores(h_q[i], h_s[i], words[:], e_planes[:, plane, :], acc[:].rearrange("p d v -> p (d v)"))
+            upper = keep.tile([P, 2, V], F32, name="upper%d_%d" % (i, side))
+            if side == 0:
+                nc.scalar.activation(out=upper[:], in_=acc[:, 2:4], func=ACT.Copy, bias=MARGIN)
+                nc.vector.scalar_tensor_tensor(out=pairs[:, i, side], in0=acc[:, 0:2], scalar=MARGIN, in1=upper[:], op0=ALU.add, op1=ALU.max)
+            else:
+                nc.scalar.activation(out=upper[:], in_=acc[:, 2:4], func=ACT.Copy, scale=-1.0)
+                nc.vector.scalar_tensor_tensor(out=pairs[:, i, side], in0=acc[:, 0:2], scalar=-1.0, in1=upper[:], op0=ALU.mult, op1=ALU.max)
 
-        def second_round_of_side(lo, hi, side):
-            nc.vector.tensor_tensor(out=best[:, lo:hi, side], in0=pairs[:, lo:hi, side, 0], in1=pairs[:, lo:hi, side, 1], op=ALU.max)
+        def best_negatives(lo, hi):
+            nc.vector.tensor_tensor(out=best[:, lo:hi], in0=pairs[:, lo:hi, 0, 0], in1=pairs[:, lo:hi, 0, 1], op=ALU.max)
 
-        def difference(lo, hi, engine):
-            engine.tensor_tensor(out=gap[:, lo:hi], in0=best[:, lo:hi, 0], in1=best[:, lo:hi, 1], op=ALU.add)
+        def turned_sums(i):
+            acc = psum.tile([P, 2, V], F32, name="turned", tag="bank")
+            for half in range(2):
+                add_turned(acc[:, half], best[:, i], half == 0, False)
+            for half in range(2):
+                add_turned(acc[:, half], pairs[:, i, 1, half], False, half == 1)
+            clipped = keep.tile([P, V], F32, name="clipped%d" % i)
+            nc.scalar.activation(out=clipped[:], in_=acc[:, 1], func=ACT.Relu)
+            return acc, clipped
+
+        loss = keep.tile([P, TILES, V], F32, name="loss")
+        sums = keep.tile([P, 2, 2, V], F32, name="sums")
+
+        def store(i):
+            queue = (nc.scalar, nc.sync)[i % 2]
+            queue.dma_start(out=out[TOK * i : TOK * (i + 1), :], in_=loss[:, i])
+
+        def finish_turned(i, acc, clipped):
+            nc.vector.tensor_tensor(out=loss[:, i], in0=acc[:, 0], in1=clipped[:], op=ALU.max)
+            store(i)
+
+        def direct_sums(i):
+            nc.vector.tensor_tensor(out=sums[:, i - TURNED], in0=pairs[:, i, 1], in1=best[:, i : i + 1].to_broadcast([P, 2, V]), op=ALU.add)
+
+        def finish_direct(i):
+            nc.vector.scalar_tensor_tensor(out=loss[:, i], in0=sums[:, i - TURNED, 0], scalar=0.0, in1=sums[:, i - TURNED, 1], op0=ALU.max, op1=ALU.max)
+            store(i)
 
         for i in range(TILES):
             first_round(i, 0)
-        second_round_of_side(0, 2, 0)
-        for i in range(2):
-            first_round(i, 1)
-        second_round_of_side(0, 1, 1)
-        difference(0, 1, nc.gpsimd)
-        second_round_of_side(2, 4, 0)
-        second_round_of_side(1, 2, 1)
-        difference(1, 2, nc.gpsimd)
+        best_negatives(0, 2)
+        first_round(0, 1)
+        first_round(1, 1)
+        best_negatives(2, 4)
         first_round(2, 1)
         first_round(3, 1)
-        for i, tag in ((0, "upper2_1"), (1, "upper3_1")):
-            early = keep.tile([P, V], F32, name="early%d" % i, tag=tag)
-            nc.scalar.activation(out=early[:], in_=gap[:, i], func=ACT.Relu)
-            nc.sync.dma_start(out=out[TOK * i : TOK * (i + 1), :], in_=early[:])
-        sums = keep.tile([P, 2, 2, V], F32, name="sums")
-        for i in (2, 3):
-            nc.vector.tensor_tensor(out=sums[:, i - 2], in0=pairs[:, i, 1], in1=best[:, i, 0:1].to_broadcast([P, 2, V]), op=ALU.add)
-        for i in (2, 3):
-            nc.vector.scalar_tensor_tensor(out=loss[:, i], in0=sums[:, i - 2, 0], scalar=0.0, in1=sums[:, i - 2, 1], op0=ALU.max, op1=ALU.max)
-            nc.sync.dma_start(out=out[TOK * i : TOK * (i + 1), :], in_=loss[:, i])
+        turned = [turned_sums(i) for i in range(TURNED)]
+        direct_sums(2)
+        finish_turned(0, *turned[0])
+        direct_sums(3)
+        finish_turned(1, *turned[1])
+        finish_direct(2)
+        finish_direct(3)

@@ -23,7 +23,7 @@ TOK = 128
 TILES = S // TOK
 V = U // D
 MARGIN = 0.3
-TURNED = 2
+TURNED = 3
 
 
 def tile_picked_yhard_hinge_p_kernel(tc, x_words, x_scales, w1, e_words, e_scales, offs, pos, neg, out):
@@ -224,7 +224,7 @@ def tile_picked_yhard_hinge_p_kernel(tc, x_words, x_scales, w1, e_words, e_scale
             return acc, clipped
 
         loss = keep.tile([P, TILES, V], F32, name="loss")
-        sums = keep.tile([P, 2, 2, V], F32, name="sums")
+        sums = keep.tile([P, TILES - TURNED, 2, V], F32, name="sums")
 
         def store(i):
             queue = (nc.scalar, nc.sync)[i % 2]
@@ -249,10 +249,15 @@ def tile_picked_yhard_hinge_p_kernel(tc, x_words, x_scales, w1, e_words, e_scale
         best_negatives(2, 4)
         first_round(2, 1)
         first_round(3, 1)
-        turned = [turned_sums(i) for i in range(TURNED)]
-        direct_sums(2)
+        turned = [turned_sums(i) for i in range(2)]
+        best_positive = keep.tile([P, V], F32, name="best_positive")
+        nc.vector.tensor_tensor(out=best_positive[:], in0=pairs[:, 2, 1, 0], in1=pairs[:, 2, 1, 1], op=ALU.max)
+        total = psum.tile([P, V], F32, name="total", tag="bank")
+        add_turned(total[:], best[:, 2], True, False)
+        add_turned(total[:], best_positive[:], False, True)
         finish_turned(0, *turned[0])
         direct_sums(3)
         finish_turned(1, *turned[1])
-        finish_direct(2)
+        nc.scalar.activation(out=loss[:, 2], in_=total[:], func=ACT.Relu)
+        store(2)
         finish_direct(3)

@@ -214,24 +214,23 @@ def tile_picked_yhard_hinge_p_kernel(tc, x_words, x_scales, w1, e_words, e_scale
             nc.vector.tensor_tensor(out=best[:, lo:hi], in0=pairs[:, lo:hi, 0, 0], in1=pairs[:, lo:hi, 0, 1], op=ALU.max)
 
         def turned_sums(i):
-            acc = psum.tile([P, 2, V], F32, name="turned", tag="bank")
+            accs = [psum.tile([P, V], F32, name="turned", tag="bank") for half in range(2)]
             for half in range(2):
-                add_turned(acc[:, half], best[:, i], half == 0, False)
-            for half in range(2):
-                add_turned(acc[:, half], pairs[:, i, 1, half], False, half == 1)
+                add_turned(accs[half][:], best[:, i], True, False)
+                add_turned(accs[half][:], pairs[:, i, 1, half], False, True)
             clipped = keep.tile([P, V], F32, name="clipped%d" % i)
-            nc.scalar.activation(out=clipped[:], in_=acc[:, 1], func=ACT.Relu)
-            return acc, clipped
+            nc.scalar.activation(out=clipped[:], in_=accs[0][:], func=ACT.Relu)
+            return accs[1], clipped
 
         loss = keep.tile([P, TILES, V], F32, name="loss")
         sums = keep.tile([P, TILES - TURNED, 2, V], F32, name="sums")
 
         def store(i):
-            queue = (nc.scalar, nc.sync)[i % 2]
+            queue = nc.scalar if i == TURNED - 1 else nc.sync
             queue.dma_start(out=out[TOK * i : TOK * (i + 1), :], in_=loss[:, i])
 
         def finish_turned(i, acc, clipped):
-            nc.vector.tensor_tensor(out=loss[:, i], in0=acc[:, 0], in1=clipped[:], op=ALU.max)
+            nc.vector.tensor_tensor(out=loss[:, i], in0=acc[:], in1=clipped[:], op=ALU.max)
             store(i)
 
         def direct_sums(i):
@@ -243,21 +242,14 @@ def tile_picked_yhard_hinge_p_kernel(tc, x_words, x_scales, w1, e_words, e_scale
 
         for i in range(TILES):
             first_round(i, 0)
-        best_negatives(0, 2)
-        first_round(0, 1)
-        first_round(1, 1)
-        best_negatives(2, 4)
-        first_round(2, 1)
+        best_negatives(0, TURNED)
+        for i in range(TURNED):
+            first_round(i, 1)
+        best_negatives(TURNED, TILES)
         first_round(3, 1)
-        turned = [turned_sums(i) for i in range(2)]
-        best_positive = keep.tile([P, V], F32, name="best_positive")
-        nc.vector.tensor_tensor(out=best_positive[:], in0=pairs[:, 2, 1, 0], in1=pairs[:, 2, 1, 1], op=ALU.max)
-        total = psum.tile([P, V], F32, name="total", tag="bank")
-        add_turned(total[:], best[:, 2], True, False)
-        add_turned(total[:], best_positive[:], False, True)
+        turned = [turned_sums(i) for i in range(TURNED)]
         finish_turned(0, *turned[0])
-        direct_sums(3)
         finish_turned(1, *turned[1])
-        nc.scalar.activation(out=loss[:, 2], in_=total[:], func=ACT.Relu)
-        store(2)
+        direct_sums(3)
+        finish_turned(2, *turned[2])
         finish_direct(3)

@@ -23,7 +23,7 @@ TOK = 128
 TILES = S // TOK
 V = U // D
 MARGIN = 0.3
-TURNED = 3
+DIRECT = 3
 
 
 def tile_picked_yhard_hinge_p_kernel(tc, x_words, x_scales, w1, e_words, e_scales, offs, pos, neg, out):
@@ -196,7 +196,7 @@ def tile_picked_yhard_hinge_p_kernel(tc, x_words, x_scales, w1, e_words, e_scale
         def first_round(i, side):
             words, plane = sides[side]
             acc = psum.tile([P, D, V], F32, name="s_acc", tag="bank")
-            if i < TURNED:
+            if i != DIRECT:
                 for d in range(D):
                     cols = slice(V * d, V * (d + 1))
                     scores(words[:, cols], e_planes[:, plane, cols], h_q[i], h_s[i], acc[:, d])
@@ -210,46 +210,54 @@ def tile_picked_yhard_hinge_p_kernel(tc, x_words, x_scales, w1, e_words, e_scale
                 nc.scalar.activation(out=upper[:], in_=acc[:, 2:4], func=ACT.Copy, scale=-1.0)
                 nc.vector.scalar_tensor_tensor(out=pairs[:, i, side], in0=acc[:, 0:2], scalar=-1.0, in1=upper[:], op0=ALU.mult, op1=ALU.max)
 
+        gap = keep.tile([P, V], F32, name="gap")
+
         def best_negatives(lo, hi):
             nc.vector.tensor_tensor(out=best[:, lo:hi], in0=pairs[:, lo:hi, 0, 0], in1=pairs[:, lo:hi, 0, 1], op=ALU.max)
 
-        def turned_sums(i):
+        def open_sums(term):
             accs = [psum.tile([P, V], F32, name="turned", tag="bank") for half in range(2)]
+            for acc in accs:
+                add_turned(acc[:], term, True, False)
+            return accs
+
+        def close_sums(i, accs, more_terms):
             for half in range(2):
-                add_turned(accs[half][:], best[:, i], True, False)
+                for term in more_terms:
+                    add_turned(accs[half][:], term, False, False)
                 add_turned(accs[half][:], pairs[:, i, 1, half], False, True)
             clipped = keep.tile([P, V], F32, name="clipped%d" % i)
             nc.scalar.activation(out=clipped[:], in_=accs[0][:], func=ACT.Relu)
             return accs[1], clipped
 
         loss = keep.tile([P, TILES, V], F32, name="loss")
-        sums = keep.tile([P, TILES - TURNED, 2, V], F32, name="sums")
+        sums = keep.tile([P, 2, V], F32, name="sums")
 
-        def store(i):
-            queue = nc.scalar if i == TURNED - 1 else nc.sync
+        def store(i, queue):
             queue.dma_start(out=out[TOK * i : TOK * (i + 1), :], in_=loss[:, i])
 
-        def finish_turned(i, acc, clipped):
+        def finish_turned(i, queue, acc, clipped):
             nc.vector.tensor_tensor(out=loss[:, i], in0=acc[:], in1=clipped[:], op=ALU.max)
-            store(i)
-
-        def direct_sums(i):
-            nc.vector.tensor_tensor(out=sums[:, i - TURNED], in0=pairs[:, i, 1], in1=best[:, i : i + 1].to_broadcast([P, 2, V]), op=ALU.add)
-
-        def finish_direct(i):
-            nc.vector.scalar_tensor_tensor(out=loss[:, i], in0=sums[:, i - TURNED, 0], scalar=0.0, in1=sums[:, i - TURNED, 1], op0=ALU.max, op1=ALU.max)
-            store(i)
+            store(i, queue)
 
         for i in range(TILES):
             first_round(i, 0)
-        best_negatives(0, TURNED)
-        for i in range(TURNED):
-            first_round(i, 1)
-        best_negatives(TURNED, TILES)
+        nc.gpsimd.tensor_tensor(out=gap[:], in0=pairs[:, 0, 0, 0], in1=pairs[:, 0, 0, 1], op=ALU.subtract)
+        best_negatives(1, 3)
+        first_round(1, 1)
+        first_round(2, 1)
+        first_round(0, 1)
+        best_negatives(3, 4)
         first_round(3, 1)
-        turned = [turned_sums(i) for i in range(TURNED)]
-        finish_turned(0, *turned[0])
-        finish_turned(1, *turned[1])
-        direct_sums(3)
-        finish_turned(2, *turned[2])
-        finish_direct(3)
+        excess = keep.tile([P, V], F32, name="excess", tag="h_bf_then_pos", align_bytes=64)
+        nc.scalar.activation(out=excess[:], in_=gap[:], func=ACT.Relu)
+        opened = {0: open_sums(pairs[:, 0, 0, 1]), 1: open_sums(best[:, 1])}
+        turned = {1: close_sums(1, opened[1], [])}
+        turned[2] = close_sums(2, open_sums(best[:, 2]), [])
+        turned[0] = close_sums(0, opened[0], [excess[:]])
+        finish_turned(1, nc.sync, *turned[1])
+        finish_turned(2, nc.sync, *turned[2])
+        nc.vector.tensor_tensor(out=sums[:], in0=pairs[:, 3, 1], in1=best[:, 3:4].to_broadcast([P, 2, V]), op=ALU.add)
+        finish_turned(0, nc.scalar, *turned[0])
+        nc.vector.scalar_tensor_tensor(out=loss[:, 3], in0=sums[:, 0], scalar=0.0, in1=sums[:, 1], op0=ALU.max, op1=ALU.max)
+        store(3, nc.sync)

@@ -24,6 +24,9 @@ TILES = S // TOK
 V = U // D
 MARGIN = 0.3
 DIRECT = 3
+X_SLICES = ((0, 128), (128, 256), (256, 384), (384, 512))
+WARM_UPS = (512, 256)
+SCORE_BANK = ((3, 4, 5, 6), (2, 7, 1, 0))
 
 
 def tile_picked_yhard_hinge_p_kernel(tc, x_words, x_scales, w1, e_words, e_scales, offs, pos, neg, out):
@@ -32,7 +35,10 @@ def tile_picked_yhard_hinge_p_kernel(tc, x_words, x_scales, w1, e_words, e_scale
         lists = ctx.enter_context(tc.tile_pool(name="lists", bufs=1))
         keep = ctx.enter_context(tc.tile_pool(name="keep", bufs=1))
         shared = ctx.enter_context(tc.tile_pool(name="shared", bufs=1))
-        psum = ctx.enter_context(tc.psum_pool(name="psum", bufs=8))
+        psum = ctx.enter_context(tc.psum_pool(name="psum", bufs=1))
+
+        def bank(b, shape, name):
+            return psum.tile(shape, F32, name=name, tag="bank%d" % b)
 
         offs_t = lists.tile([P, S // 16], U16, name="offs_t")
         neg_t = lists.tile([P, U // 16], U16, name="neg_t")
@@ -67,7 +73,7 @@ def tile_picked_yhard_hinge_p_kernel(tc, x_words, x_scales, w1, e_words, e_scale
         load_words(xw_all[0], x_words[0])
 
         xs_g = keep.tile([P, S], U8, name="xs_g", align_bytes=64)
-        es_g = keep.tile([P, 2, U], U8, name="es_g", align_bytes=64)
+        es_g = shared.tile([P, 2, U], U8, name="es_g", offset=18432, align_bytes=64)
         nc.vector.tensor_copy(xs_g[:], xs_all[:].indirect(offs_t[:]))
         w_bf = [keep.tile([P, PACK, P, PACK], BF16, name="w_bf%d" % o, align_bytes=64) for o in range(PASSES)]
 
@@ -90,8 +96,8 @@ def tile_picked_yhard_hinge_p_kernel(tc, x_words, x_scales, w1, e_words, e_scale
         e_planes = shared.tile([P, 2, U], U8, name="e_planes", offset=8192, align_bytes=64)
         nc.gpsimd.memset(e_planes[:].rearrange("p a n -> p (a n)").bitcast(I32), 0)
         load_words(ew_all, e_words[0])
-        nc.vector.tensor_copy(es_g[:, 0, :], es_all[:].indirect(neg_t[:]))
-        nc.vector.tensor_copy(es_g[:, 1, :], es_all[:].indirect(pos_t[:]))
+        for side, picks in enumerate((neg_t, pos_t)):
+            nc.vector.tensor_copy(es_g[:, side, :].rearrange("p (d v) -> p v d", d=D), es_all[:].indirect(picks[:]))
 
         w_q = []
         w_s = []
@@ -103,75 +109,84 @@ def tile_picked_yhard_hinge_p_kernel(tc, x_words, x_scales, w1, e_words, e_scale
             nc.vector.quantize_mx(out=w_q[o][:].bitcast(FP8X4), scales=w_s[o][:], in_=w_bf[o][:].rearrange("p t m j -> p (t m j)"))
 
         quantize_w(0, "wq0", "ws0")
-        es_m = shared.tile([P, 2, U], U8, name="es_m", offset=9216, align_bytes=64)
-        nc.vector.tensor_copy(es_m[:].rearrange("p a (d v) -> p a d v", d=D), es_g[:].rearrange("p a (v d) -> p a d v", d=D))
         for q in range(4):
             nc.sync.dma_start(
                 out=e_planes[32 * q : 32 * q + 4].rearrange("p a n -> p (a n)").bitcast(I32),
-                in_=es_m[32 * q : 32 * q + 32 : 8, :, :].rearrange("p a n -> p (a n)").bitcast(I32),
+                in_=es_g[32 * q : 32 * q + 32 : 8, :, :].rearrange("p a n -> p (a n)").bitcast(I32),
             )
         xw_g = [keep.tile([P, S], U32, name="xw_g%d" % o, align_bytes=64) for o in range(PASSES)]
-        nc.vector.tensor_copy(xw_g[0][:], xw_all[0][:].bitcast(U32).indirect(offs_t[:]))
-        quantize_w(1, "wq1", "ws1")
-        for half in range(2):
-            nc.vector.tensor_copy(
-                xw_g[1][:, 256 * half : 256 * (half + 1)],
-                xw_all[1][:].bitcast(U32).indirect(offs_t[:, 16 * half : 16 * (half + 1)]),
-            )
 
-        def warm_up(t, words, scales):
-            idle = psum.tile([P, S], F32, name="idle", tag="bank")
+        def gather_x(o):
+            for lo, hi in X_SLICES:
+                nc.vector.tensor_copy(xw_g[o][:, lo:hi], xw_all[o][:].bitcast(U32).indirect(offs_t[:, lo // 16 : hi // 16]))
+
+        gather_x(0)
+        quantize_w(1, "wq1", "ws1")
+        gather_x(1)
+
+        h_bf0 = keep.tile([P, 1, TOK, PACK], BF16, name="h_bf0", align_bytes=64)
+        h_bf12 = keep.tile([P, 2, TOK, PACK], BF16, name="h_bf12", tag="h_bf_then_pos", align_bytes=64)
+        h_bf3 = keep.tile([P, 1, TOK, PACK], BF16, name="h_bf3", align_bytes=64)
+        h_bf = [h_bf0[:, 0], h_bf12[:, 0], h_bf12[:, 1], h_bf3[:, 0]]
+
+        def project(acc, i, o):
+            for t in range(PACK):
+                ch = slice(P * t, P * (t + 1))
+                nc.tensor.matmul_mx(
+                    out=acc[:, t, :],
+                    lhsT=w_q[o][:, ch].bitcast(FP8X4),
+                    lhsT_scale=w_s[o][:, ch],
+                    rhs=xw_g[o][:, TOK * i : TOK * (i + 1)].bitcast(FP8X4),
+                    rhs_scale=planes[:, o, TOK * i : TOK * (i + 1)],
+                    start=(o == 0 and t == 0),
+                    stop=(o == PASSES - 1 and t == PACK - 1),
+                )
+
+        def round_h(acc, i):
+            nc.scalar.copy(out=h_bf[i], in_=acc[:].rearrange("p t n -> p n t"))
+
+        for t, width in enumerate(WARM_UPS):
+            idle = bank(3 + t, [P, width], "idle")
             nc.tensor.matmul_mx(
                 out=idle[:],
                 lhsT=w_q[0][:, P * t : P * (t + 1)].bitcast(FP8X4),
                 lhsT_scale=w_s[0][:, P * t : P * (t + 1)],
-                rhs=words.bitcast(FP8X4),
-                rhs_scale=scales,
+                rhs=w_q[0][:, 0:width].bitcast(FP8X4),
+                rhs_scale=w_s[0][:, 0:width],
                 start=True,
                 stop=True,
             )
 
-        for t in range(2):
-            warm_up(t, w_q[0][:], w_s[0][:])
-
-        h_acc = [psum.tile([P, PACK, TOK], F32, name="h_acc%d" % i, tag="bank") for i in range(TILES)]
+        h_acc = [bank(i, [P, PACK, TOK], "h_acc%d" % i) for i in range(TILES - 1)]
         for o in range(PASSES):
-            for i in range(TILES):
-                tok = slice(TOK * i, TOK * (i + 1))
-                for t in range(PACK):
-                    ch = slice(P * t, P * (t + 1))
-                    nc.tensor.matmul_mx(
-                        out=h_acc[i][:, t, :],
-                        lhsT=w_q[o][:, ch].bitcast(FP8X4),
-                        lhsT_scale=w_s[o][:, ch],
-                        rhs=xw_g[o][:, tok].bitcast(FP8X4),
-                        rhs_scale=planes[:, o, tok],
-                        start=(o == 0 and t == 0),
-                        stop=(o == PASSES - 1 and t == PACK - 1),
-                    )
+            for i in range(TILES - 1):
+                project(h_acc[i], i, o)
+        for i in range(TILES - 1):
+            round_h(h_acc[i], i)
+        last = bank(0, [P, PACK, TOK], "h_acc_last")
+        for o in range(PASSES):
+            project(last, TILES - 1, o)
+        round_h(last, TILES - 1)
 
-        for t in range(2):
-            warm_up(t, xw_g[0][:], e_planes[:, 0, :])
+        h_codes0 = keep.tile([P, 1, TOK], U32, name="h_codes0", align_bytes=64)
+        h_scales0 = keep.tile([P, 1, TOK], U8, name="h_scales0", align_bytes=64)
+        h_codes123 = keep.tile([P, 3, TOK], U32, name="h_codes123", align_bytes=64)
+        h_scales123 = shared.tile([P, 3, TOK], U8, name="h_scales123", offset=18432, align_bytes=64)
+        h_q = [h_codes0[:, 0]] + [h_codes123[:, i] for i in range(3)]
+        h_s = [h_scales0[:, 0]] + [h_scales123[:, i] for i in range(3)]
 
-        h_bf01 = keep.tile([P, 2, TOK, PACK], BF16, name="h_bf01", tag="h_bf_then_pos", align_bytes=64)
-        h_bf23 = keep.tile([P, 2, TOK, PACK], BF16, name="h_bf23", align_bytes=64)
-        nc.vector.tensor_copy(out=h_bf01[:, 0], in_=h_acc[0][:].rearrange("p t n -> p n t"))
-        for i in range(1, TILES):
-            nc.scalar.copy(out=(h_bf01, h_bf23)[i // 2][:, i % 2], in_=h_acc[i][:].rearrange("p t n -> p n t"))
-
-        h_codes = keep.tile([P, TILES, TOK], U32, name="h_codes", align_bytes=64)
-        h_scales = shared.tile([P, TILES, TOK], U8, name="h_scales", offset=9216, align_bytes=64)
-        h_q = [h_codes[:, i] for i in range(TILES)]
-        h_s = [h_scales[:, i] for i in range(TILES)]
-
-        nw_g = keep.tile([P, U], U32, name="nw_g", align_bytes=64)
-        nc.vector.tensor_copy(nw_g[:].rearrange("p (d v) -> p v d", d=D), ew_all[:].bitcast(U32).indirect(neg_t[:]))
-        for g, values in enumerate((h_bf01, h_bf23)):
+        def quantize_h(codes, scales, values):
             nc.vector.quantize_mx(
-                out=h_codes[:, 2 * g : 2 * g + 2].rearrange("p i n -> p (i n)").bitcast(FP8X4),
-                scales=h_scales[:, 2 * g : 2 * g + 2].rearrange("p i n -> p (i n)"),
+                out=codes.rearrange("p i n -> p (i n)").bitcast(FP8X4),
+                scales=scales.rearrange("p i n -> p (i n)"),
                 in_=values[:].rearrange("p i n t -> p (i n t)"),
             )
+
+        quantize_h(h_codes0[:], h_scales0[:], h_bf0)
+        nw_g = keep.tile([P, U], U32, name="nw_g", align_bytes=64)
+        nc.vector.tensor_copy(nw_g[:].rearrange("p (d v) -> p v d", d=D), ew_all[:].bitcast(U32).indirect(neg_t[:]))
+        quantize_h(h_codes123[:, 0:2], h_scales123[:, 0:2], h_bf12)
+        quantize_h(h_codes123[:, 2:3], h_scales123[:, 2:3], h_bf3)
         pw_g = keep.tile([P, U], U32, name="pw_g", tag="h_bf_then_pos", align_bytes=64)
         nc.vector.tensor_copy(pw_g[:].rearrange("p (d v) -> p v d", d=D), ew_all[:].bitcast(U32).indirect(pos_t[:]))
 
@@ -195,7 +210,7 @@ def tile_picked_yhard_hinge_p_kernel(tc, x_words, x_scales, w1, e_words, e_scale
 
         def first_round(i, side):
             words, plane = sides[side]
-            acc = psum.tile([P, D, V], F32, name="s_acc", tag="bank")
+            acc = bank(SCORE_BANK[side][i], [P, D, V], "s_acc")
             if i != DIRECT:
                 for d in range(D):
                     cols = slice(V * d, V * (d + 1))
@@ -215,8 +230,8 @@ def tile_picked_yhard_hinge_p_kernel(tc, x_words, x_scales, w1, e_words, e_scale
         def best_negatives(lo, hi):
             nc.vector.tensor_tensor(out=best[:, lo:hi], in0=pairs[:, lo:hi, 0, 0], in1=pairs[:, lo:hi, 0, 1], op=ALU.max)
 
-        def open_sums(term):
-            accs = [psum.tile([P, V], F32, name="turned", tag="bank") for half in range(2)]
+        def open_sums(term, banks):
+            accs = [bank(b, [P, V], "turned") for b in banks]
             for acc in accs:
                 add_turned(acc[:], term, True, False)
             return accs
@@ -251,9 +266,9 @@ def tile_picked_yhard_hinge_p_kernel(tc, x_words, x_scales, w1, e_words, e_scale
         first_round(3, 1)
         excess = keep.tile([P, V], F32, name="excess", tag="h_bf_then_pos", align_bytes=64)
         nc.scalar.activation(out=excess[:], in_=gap[:], func=ACT.Relu)
-        opened = {0: open_sums(pairs[:, 0, 0, 1]), 1: open_sums(best[:, 1])}
+        opened = {0: open_sums(pairs[:, 0, 0, 1], (3, 4)), 1: open_sums(best[:, 1], (5, 6))}
         turned = {1: close_sums(1, opened[1], [])}
-        turned[2] = close_sums(2, open_sums(best[:, 2]), [])
+        turned[2] = close_sums(2, open_sums(best[:, 2], (7, 1)), [])
         turned[0] = close_sums(0, opened[0], [excess[:]])
         finish_turned(1, nc.sync, *turned[1])
         finish_turned(2, nc.sync, *turned[2])

@@ -24,9 +24,9 @@ TILES = S // TOK
 V = U // D
 MARGIN = 0.3
 DIRECT = 3
-X_SLICES = ((0, 128), (128, 256), (256, 384), (384, 512))
+X_SLICES = ((0, 128), (128, 256), (256, 512))
 WARM_UPS = (512, 256)
-SCORE_BANK = ((3, 4, 5, 6), (2, 7, 1, 0))
+SCORE_BANK = ((4, 5, 6, 7), (2, 0, 1, 3))
 
 
 def tile_picked_yhard_hinge_p_kernel(tc, x_words, x_scales, w1, e_words, e_scales, offs, pos, neg, out):
@@ -124,10 +124,9 @@ def tile_picked_yhard_hinge_p_kernel(tc, x_words, x_scales, w1, e_words, e_scale
         quantize_w(1, "wq1", "ws1")
         gather_x(1)
 
-        h_bf0 = keep.tile([P, 1, TOK, PACK], BF16, name="h_bf0", align_bytes=64)
-        h_bf12 = keep.tile([P, 2, TOK, PACK], BF16, name="h_bf12", tag="h_bf_then_pos", align_bytes=64)
-        h_bf3 = keep.tile([P, 1, TOK, PACK], BF16, name="h_bf3", align_bytes=64)
-        h_bf = [h_bf0[:, 0], h_bf12[:, 0], h_bf12[:, 1], h_bf3[:, 0]]
+        h_bf01 = keep.tile([P, 2, TOK, PACK], BF16, name="h_bf01", tag="h_bf_then_pos", align_bytes=64)
+        h_bf23 = keep.tile([P, 2, TOK, PACK], BF16, name="h_bf23", align_bytes=64)
+        h_bf = [h_bf01[:, 0], h_bf01[:, 1], h_bf23[:, 0], h_bf23[:, 1]]
 
         def project(acc, i, o):
             for t in range(PACK):
@@ -143,37 +142,33 @@ def tile_picked_yhard_hinge_p_kernel(tc, x_words, x_scales, w1, e_words, e_scale
                 )
 
         def round_h(acc, i):
-            nc.scalar.copy(out=h_bf[i], in_=acc[:].rearrange("p t n -> p n t"))
+            copy = nc.vector.tensor_copy if i == 0 else nc.scalar.copy
+            copy(out=h_bf[i], in_=acc[:].rearrange("p t n -> p n t"))
+
+        h_acc = [bank(i, [P, PACK, TOK], "h_acc%d" % i) for i in range(TILES)]
+        for o in range(PASSES):
+            for i in range(TILES):
+                project(h_acc[i], i, o)
 
         for t, width in enumerate(WARM_UPS):
-            idle = bank(3 + t, [P, width], "idle")
+            idle = bank(4 + t, [P, width], "idle")
             nc.tensor.matmul_mx(
                 out=idle[:],
                 lhsT=w_q[0][:, P * t : P * (t + 1)].bitcast(FP8X4),
                 lhsT_scale=w_s[0][:, P * t : P * (t + 1)],
                 rhs=w_q[0][:, 0:width].bitcast(FP8X4),
-                rhs_scale=w_s[0][:, 0:width],
+                rhs_scale=e_planes[:, 0, 0:width],
                 start=True,
                 stop=True,
             )
 
-        h_acc = [bank(i, [P, PACK, TOK], "h_acc%d" % i) for i in range(TILES - 1)]
-        for o in range(PASSES):
-            for i in range(TILES - 1):
-                project(h_acc[i], i, o)
-        for i in range(TILES - 1):
+        for i in range(TILES):
             round_h(h_acc[i], i)
-        last = bank(0, [P, PACK, TOK], "h_acc_last")
-        for o in range(PASSES):
-            project(last, TILES - 1, o)
-        round_h(last, TILES - 1)
 
-        h_codes0 = keep.tile([P, 1, TOK], U32, name="h_codes0", align_bytes=64)
-        h_scales0 = keep.tile([P, 1, TOK], U8, name="h_scales0", align_bytes=64)
-        h_codes123 = keep.tile([P, 3, TOK], U32, name="h_codes123", align_bytes=64)
-        h_scales123 = shared.tile([P, 3, TOK], U8, name="h_scales123", offset=18432, align_bytes=64)
-        h_q = [h_codes0[:, 0]] + [h_codes123[:, i] for i in range(3)]
-        h_s = [h_scales0[:, 0]] + [h_scales123[:, i] for i in range(3)]
+        h_codes = keep.tile([P, TILES, TOK], U32, name="h_codes", align_bytes=64)
+        h_scales = shared.tile([P, TILES, TOK], U8, name="h_scales", offset=18432, align_bytes=64)
+        h_q = [h_codes[:, i] for i in range(TILES)]
+        h_s = [h_scales[:, i] for i in range(TILES)]
 
         def quantize_h(codes, scales, values):
             nc.vector.quantize_mx(
@@ -182,11 +177,10 @@ def tile_picked_yhard_hinge_p_kernel(tc, x_words, x_scales, w1, e_words, e_scale
                 in_=values[:].rearrange("p i n t -> p (i n t)"),
             )
 
-        quantize_h(h_codes0[:], h_scales0[:], h_bf0)
         nw_g = keep.tile([P, U], U32, name="nw_g", align_bytes=64)
         nc.vector.tensor_copy(nw_g[:].rearrange("p (d v) -> p v d", d=D), ew_all[:].bitcast(U32).indirect(neg_t[:]))
-        quantize_h(h_codes123[:, 0:2], h_scales123[:, 0:2], h_bf12)
-        quantize_h(h_codes123[:, 2:3], h_scales123[:, 2:3], h_bf3)
+        quantize_h(h_codes[:, 0:2], h_scales[:, 0:2], h_bf01)
+        quantize_h(h_codes[:, 2:4], h_scales[:, 2:4], h_bf23)
         pw_g = keep.tile([P, U], U32, name="pw_g", tag="h_bf_then_pos", align_bytes=64)
         nc.vector.tensor_copy(pw_g[:].rearrange("p (d v) -> p v d", d=D), ew_all[:].bitcast(U32).indirect(pos_t[:]))
 
@@ -266,9 +260,9 @@ def tile_picked_yhard_hinge_p_kernel(tc, x_words, x_scales, w1, e_words, e_scale
         first_round(3, 1)
         excess = keep.tile([P, V], F32, name="excess", tag="h_bf_then_pos", align_bytes=64)
         nc.scalar.activation(out=excess[:], in_=gap[:], func=ACT.Relu)
-        opened = {0: open_sums(pairs[:, 0, 0, 1], (3, 4)), 1: open_sums(best[:, 1], (5, 6))}
+        opened = {0: open_sums(pairs[:, 0, 0, 1], (4, 5)), 1: open_sums(best[:, 1], (6, 7))}
         turned = {1: close_sums(1, opened[1], [])}
-        turned[2] = close_sums(2, open_sums(best[:, 2], (7, 1)), [])
+        turned[2] = close_sums(2, open_sums(best[:, 2], (0, 1)), [])
         turned[0] = close_sums(0, opened[0], [excess[:]])
         finish_turned(1, nc.sync, *turned[1])
         finish_turned(2, nc.sync, *turned[2])

@@ -72,7 +72,7 @@ def tile_picked_yhard_hinge_p_kernel(tc, x_words, x_scales, w1, e_words, e_scale
         xw_all = [keep.tile([P, T], I32, name="xw_all0", tag="xw0", align_bytes=64)]
         load_words(xw_all[0], x_words[0])
 
-        xs_g = keep.tile([P, S], U8, name="xs_g", align_bytes=64)
+        xs_g = shared.tile([P, S], U8, name="xs_g", offset=19456, align_bytes=64)
         es_g = shared.tile([P, 2, U], U8, name="es_g", offset=18432, align_bytes=64)
         nc.vector.tensor_copy(xs_g[:], xs_all[:].indirect(offs_t[:]))
         w_bf = [keep.tile([P, PACK, P, PACK], BF16, name="w_bf%d" % o, align_bytes=64) for o in range(PASSES)]
@@ -86,7 +86,7 @@ def tile_picked_yhard_hinge_p_kernel(tc, x_words, x_scales, w1, e_words, e_scale
 
         cast_w(0)
         for q in range(4):
-            nc.scalar.dma_start(
+            nc.sync.dma_start(
                 out=planes[32 * q : 32 * q + 4].rearrange("p a n -> p (a n)").bitcast(I32),
                 in_=xs_g[32 * q : 32 * q + 32 : 4, :].bitcast(I32),
             )
@@ -103,12 +103,12 @@ def tile_picked_yhard_hinge_p_kernel(tc, x_words, x_scales, w1, e_words, e_scale
         w_s = []
         cast_w(1)
 
-        def quantize_w(o, codes_tag, scales_tag):
-            w_q.append(keep.tile([P, H], U32, name="w_q%d" % o, tag=codes_tag, align_bytes=64))
-            w_s.append(keep.tile([P, H], U8, name="w_s%d" % o, tag=scales_tag, align_bytes=64))
+        def quantize_w(o, scales_offset):
+            w_q.append(keep.tile([P, H], U32, name="w_q%d" % o, align_bytes=64))
+            w_s.append(shared.tile([P, H], U8, name="w_s%d" % o, offset=scales_offset, align_bytes=64))
             nc.vector.quantize_mx(out=w_q[o][:].bitcast(FP8X4), scales=w_s[o][:], in_=w_bf[o][:].rearrange("p t m j -> p (t m j)"))
 
-        quantize_w(0, "wq0", "ws0")
+        quantize_w(0, 19968)
         for q in range(4):
             nc.sync.dma_start(
                 out=e_planes[32 * q : 32 * q + 4].rearrange("p a n -> p (a n)").bitcast(I32),
@@ -121,12 +121,13 @@ def tile_picked_yhard_hinge_p_kernel(tc, x_words, x_scales, w1, e_words, e_scale
                 nc.vector.tensor_copy(xw_g[o][:, lo:hi], xw_all[o][:].bitcast(U32).indirect(offs_t[:, lo // 16 : hi // 16]))
 
         gather_x(0)
-        quantize_w(1, "wq1", "ws1")
+        quantize_w(1, 19456)
         gather_x(1)
 
-        h_bf01 = keep.tile([P, 2, TOK, PACK], BF16, name="h_bf01", tag="h_bf_then_pos", align_bytes=64)
-        h_bf23 = keep.tile([P, 2, TOK, PACK], BF16, name="h_bf23", align_bytes=64)
-        h_bf = [h_bf01[:, 0], h_bf01[:, 1], h_bf23[:, 0], h_bf23[:, 1]]
+        h_bf0 = keep.tile([P, 1, TOK, PACK], BF16, name="h_bf0", align_bytes=64)
+        h_bf12 = keep.tile([P, 2, TOK, PACK], BF16, name="h_bf12", tag="h_bf_then_pos", align_bytes=64)
+        h_bf3 = keep.tile([P, 1, TOK, PACK], BF16, name="h_bf3", align_bytes=64)
+        h_bf = [h_bf0[:, 0], h_bf12[:, 0], h_bf12[:, 1], h_bf3[:, 0]]
 
         def project(acc, i, o):
             for t in range(PACK):
@@ -141,9 +142,8 @@ def tile_picked_yhard_hinge_p_kernel(tc, x_words, x_scales, w1, e_words, e_scale
                     stop=(o == PASSES - 1 and t == PACK - 1),
                 )
 
-        def round_h(acc, i):
-            copy = nc.vector.tensor_copy if i == 0 else nc.scalar.copy
-            copy(out=h_bf[i], in_=acc[:].rearrange("p t n -> p n t"))
+        def round_h(copy, i, lo, hi):
+            copy(out=h_bf[i][:, lo:hi], in_=h_acc[i][:, :, lo:hi].rearrange("p t n -> p n t"))
 
         h_acc = [bank(i, [P, PACK, TOK], "h_acc%d" % i) for i in range(TILES)]
         for o in range(PASSES):
@@ -162,13 +162,18 @@ def tile_picked_yhard_hinge_p_kernel(tc, x_words, x_scales, w1, e_words, e_scale
                 stop=True,
             )
 
-        for i in range(TILES):
-            round_h(h_acc[i], i)
+        round_h(nc.scalar.copy, 0, 0, TOK)
+        round_h(nc.vector.tensor_copy, 1, 0, TOK // 2)
+        round_h(nc.scalar.copy, 2, 0, TOK)
+        round_h(nc.scalar.copy, 1, TOK // 2, TOK)
+        round_h(nc.scalar.copy, 3, 0, TOK)
 
-        h_codes = keep.tile([P, TILES, TOK], U32, name="h_codes", align_bytes=64)
-        h_scales = shared.tile([P, TILES, TOK], U8, name="h_scales", offset=18432, align_bytes=64)
-        h_q = [h_codes[:, i] for i in range(TILES)]
-        h_s = [h_scales[:, i] for i in range(TILES)]
+        h_codes0 = keep.tile([P, 1, TOK], U32, name="h_codes0", align_bytes=64)
+        h_scales0 = keep.tile([P, 1, TOK], U8, name="h_scales0", align_bytes=64)
+        h_codes123 = keep.tile([P, 3, TOK], U32, name="h_codes123", align_bytes=64)
+        h_scales123 = shared.tile([P, 3, TOK], U8, name="h_scales123", offset=18432, align_bytes=64)
+        h_q = [h_codes0[:, 0]] + [h_codes123[:, i] for i in range(3)]
+        h_s = [h_scales0[:, 0]] + [h_scales123[:, i] for i in range(3)]
 
         def quantize_h(codes, scales, values):
             nc.vector.quantize_mx(
@@ -177,10 +182,11 @@ def tile_picked_yhard_hinge_p_kernel(tc, x_words, x_scales, w1, e_words, e_scale
                 in_=values[:].rearrange("p i n t -> p (i n t)"),
             )
 
+        quantize_h(h_codes0[:], h_scales0[:], h_bf0)
         nw_g = keep.tile([P, U], U32, name="nw_g", align_bytes=64)
         nc.vector.tensor_copy(nw_g[:].rearrange("p (d v) -> p v d", d=D), ew_all[:].bitcast(U32).indirect(neg_t[:]))
-        quantize_h(h_codes[:, 0:2], h_scales[:, 0:2], h_bf01)
-        quantize_h(h_codes[:, 2:4], h_scales[:, 2:4], h_bf23)
+        quantize_h(h_codes123[:, 0:2], h_scales123[:, 0:2], h_bf12)
+        quantize_h(h_codes123[:, 2:3], h_scales123[:, 2:3], h_bf3)
         pw_g = keep.tile([P, U], U32, name="pw_g", tag="h_bf_then_pos", align_bytes=64)
         nc.vector.tensor_copy(pw_g[:].rearrange("p (d v) -> p v d", d=D), ew_all[:].bitcast(U32).indirect(pos_t[:]))
 

@@ -44,17 +44,19 @@ def tile_picked_yhard_hinge_p_kernel(tc, x_words, x_scales, w1, e_words, e_scale
         neg_t = lists.tile([P, U // 16], U16, name="neg_t")
         pos_t = lists.tile([P, U // 16], U16, name="pos_t")
 
-        xs_all = keep.tile([P, T], U8, name="xs_all", align_bytes=64)
-        es_all = keep.tile([P, T], U8, name="es_all", align_bytes=64)
+        xs_all = shared.tile([P, T], U8, name="xs_all", offset=0, align_bytes=64)
+        es_all = shared.tile([P, T], U8, name="es_all", offset=8192, align_bytes=64)
         planes = keep.tile([P, 2, S], U8, name="planes", align_bytes=64)
         nc.vector.memset(xs_all[:].bitcast(I32), 0)
-        nc.vector.memset(es_all[:].bitcast(I32), 0)
+        nc.gpsimd.memset(es_all[:].bitcast(I32), 0)
         nc.vector.memset(planes[:].rearrange("p a n -> p (a n)").bitcast(I32), 0)
+        e_planes = keep.tile([P, 2, U], U8, name="e_planes", align_bytes=64)
+        nc.vector.memset(e_planes[:].rearrange("p a n -> p (a n)").bitcast(I32), 0)
 
         identity = keep.tile([P, P], F32, name="identity")
         make_identity(nc, identity[:])
 
-        w_raw = [shared.tile([P, PACK, H], F32, name="w_raw0", offset=4096, align_bytes=64), keep.tile([P, PACK, H], F32, name="w_raw1")]
+        w_raw = [keep.tile([P, PACK, H], F32, name="w_raw%d" % o) for o in range(PASSES)]
 
         def load_w(o):
             nc.sync.dma_start(out=w_raw[o][:], in_=w1[512 * o : 512 * (o + 1), :].rearrange("(p j) c -> p j c", j=PACK))
@@ -92,12 +94,10 @@ def tile_picked_yhard_hinge_p_kernel(tc, x_words, x_scales, w1, e_words, e_scale
             )
         xw_all.append(shared.tile([P, T], I32, name="xw_all1", offset=0, align_bytes=64))
         load_words(xw_all[1], x_words[1])
-        ew_all = shared.tile([P, T], I32, name="ew_all", offset=10240, align_bytes=64)
-        e_planes = shared.tile([P, 2, U], U8, name="e_planes", offset=8192, align_bytes=64)
-        nc.gpsimd.memset(e_planes[:].rearrange("p a n -> p (a n)").bitcast(I32), 0)
-        load_words(ew_all, e_words[0])
+        ew_all = shared.tile([P, T], I32, name="ew_all", offset=8192, align_bytes=64)
         for side, picks in enumerate((neg_t, pos_t)):
             nc.vector.tensor_copy(es_g[:, side, :].rearrange("p (d v) -> p v d", d=D), es_all[:].indirect(picks[:]))
+        load_words(ew_all, e_words[0])
 
         w_q = []
         w_s = []

@@ -75,7 +75,7 @@ def tile_picked_yhard_hinge_p_kernel(tc, x_words, x_scales, w1, e_words, e_scale
         load_words(xw_all[0], x_words[0])
 
         xs_g = shared.tile([P, S], U8, name="xs_g", offset=19456, align_bytes=64)
-        es_g = shared.tile([P, 2, U], U8, name="es_g", offset=18432, align_bytes=64)
+        es_g = shared.tile([P, 2, U], U8, name="es_g", offset=24576, align_bytes=64)
         nc.vector.tensor_copy(xs_g[:], xs_all[:].indirect(offs_t[:]))
         w_bf = [keep.tile([P, PACK, P, PACK], BF16, name="w_bf%d" % o, align_bytes=64) for o in range(PASSES)]
 
@@ -125,9 +125,9 @@ def tile_picked_yhard_hinge_p_kernel(tc, x_words, x_scales, w1, e_words, e_scale
         gather_x(1)
 
         h_bf0 = keep.tile([P, 1, TOK, PACK], BF16, name="h_bf0", align_bytes=64)
-        h_bf12 = keep.tile([P, 2, TOK, PACK], BF16, name="h_bf12", tag="h_bf_then_pos", align_bytes=64)
-        h_bf3 = keep.tile([P, 1, TOK, PACK], BF16, name="h_bf3", align_bytes=64)
-        h_bf = [h_bf0[:, 0], h_bf12[:, 0], h_bf12[:, 1], h_bf3[:, 0]]
+        h_bf1 = keep.tile([P, 1, TOK, PACK], BF16, name="h_bf1", align_bytes=64)
+        h_bf23 = keep.tile([P, 2, TOK, PACK], BF16, name="h_bf23", align_bytes=64)
+        h_bf = [h_bf0[:, 0], h_bf1[:, 0], h_bf23[:, 0], h_bf23[:, 1]]
 
         def project(acc, i, o):
             for t in range(PACK):
@@ -163,17 +163,15 @@ def tile_picked_yhard_hinge_p_kernel(tc, x_words, x_scales, w1, e_words, e_scale
             )
 
         round_h(nc.scalar.copy, 0, 0, TOK)
-        round_h(nc.vector.tensor_copy, 1, 0, TOK // 2)
+        round_h(nc.vector.tensor_copy, 1, 0, TOK)
         round_h(nc.scalar.copy, 2, 0, TOK)
-        round_h(nc.scalar.copy, 1, TOK // 2, TOK)
         round_h(nc.scalar.copy, 3, 0, TOK)
 
-        h_codes0 = keep.tile([P, 1, TOK], U32, name="h_codes0", align_bytes=64)
-        h_scales0 = keep.tile([P, 1, TOK], U8, name="h_scales0", align_bytes=64)
-        h_codes123 = keep.tile([P, 3, TOK], U32, name="h_codes123", align_bytes=64)
-        h_scales123 = shared.tile([P, 3, TOK], U8, name="h_scales123", offset=18432, align_bytes=64)
-        h_q = [h_codes0[:, 0]] + [h_codes123[:, i] for i in range(3)]
-        h_s = [h_scales0[:, 0]] + [h_scales123[:, i] for i in range(3)]
+        h_codes = keep.tile([P, TILES, TOK], U32, name="h_codes", align_bytes=64)
+        h_scales01 = keep.tile([P, 2, TOK], U8, name="h_scales01", align_bytes=64)
+        h_scales23 = shared.tile([P, 2, TOK], U8, name="h_scales23", offset=24576, align_bytes=64)
+        h_q = [h_codes[:, i] for i in range(TILES)]
+        h_s = [h_scales01[:, 0], h_scales01[:, 1], h_scales23[:, 0], h_scales23[:, 1]]
 
         def quantize_h(codes, scales, values):
             nc.vector.quantize_mx(
@@ -182,12 +180,12 @@ def tile_picked_yhard_hinge_p_kernel(tc, x_words, x_scales, w1, e_words, e_scale
                 in_=values[:].rearrange("p i n t -> p (i n t)"),
             )
 
-        quantize_h(h_codes0[:], h_scales0[:], h_bf0)
+        quantize_h(h_codes[:, 0:1], h_scales01[:, 0:1], h_bf0)
+        quantize_h(h_codes[:, 1:2], h_scales01[:, 1:2], h_bf1)
         nw_g = keep.tile([P, U], U32, name="nw_g", align_bytes=64)
         nc.vector.tensor_copy(nw_g[:].rearrange("p (d v) -> p v d", d=D), ew_all[:].bitcast(U32).indirect(neg_t[:]))
-        quantize_h(h_codes123[:, 0:2], h_scales123[:, 0:2], h_bf12)
-        quantize_h(h_codes123[:, 2:3], h_scales123[:, 2:3], h_bf3)
-        pw_g = keep.tile([P, U], U32, name="pw_g", tag="h_bf_then_pos", align_bytes=64)
+        quantize_h(h_codes[:, 2:4], h_scales23[:], h_bf23)
+        pw_g = shared.tile([P, U], U32, name="pw_g", offset=25088, align_bytes=64)
         nc.vector.tensor_copy(pw_g[:].rearrange("p (d v) -> p v d", d=D), ew_all[:].bitcast(U32).indirect(pos_t[:]))
 
         def scores(lhsT, lhsT_scale, rhs, rhs_scale, acc):
@@ -264,7 +262,7 @@ def tile_picked_yhard_hinge_p_kernel(tc, x_words, x_scales, w1, e_words, e_scale
         first_round(0, 1)
         best_negatives(3, 4)
         first_round(3, 1)
-        excess = keep.tile([P, V], F32, name="excess", tag="h_bf_then_pos", align_bytes=64)
+        excess = shared.tile([P, V], F32, name="excess", offset=25088, align_bytes=64)
         nc.scalar.activation(out=excess[:], in_=gap[:], func=ACT.Relu)
         opened = {0: open_sums(pairs[:, 0, 0, 1], (4, 5)), 1: open_sums(best[:, 1], (6, 7))}
         turned = {1: close_sums(1, opened[1], [])}

@@ -26,7 +26,7 @@ MARGIN = 0.3
 DIRECT = 3
 X_SLICES = ((0, 128), (128, 256), (256, 512))
 WARM_UPS = (512, 256)
-SCORE_BANK = ((4, 5, 6, 7), (2, 0, 1, 3))
+SCORE_BANK = ((4, 5, 6, 7), (2, 3, 1, 0))
 
 
 def tile_picked_yhard_hinge_p_kernel(tc, x_words, x_scales, w1, e_words, e_scales, offs, pos, neg, out):
@@ -145,11 +145,6 @@ def tile_picked_yhard_hinge_p_kernel(tc, x_words, x_scales, w1, e_words, e_scale
         def round_h(copy, i, lo, hi):
             copy(out=h_bf[i][:, lo:hi], in_=h_acc[i][:, :, lo:hi].rearrange("p t n -> p n t"))
 
-        h_acc = [bank(i, [P, PACK, TOK], "h_acc%d" % i) for i in range(TILES)]
-        for o in range(PASSES):
-            for i in range(TILES):
-                project(h_acc[i], i, o)
-
         for t, width in enumerate(WARM_UPS):
             idle = bank(4 + t, [P, width], "idle")
             nc.tensor.matmul_mx(
@@ -157,14 +152,21 @@ def tile_picked_yhard_hinge_p_kernel(tc, x_words, x_scales, w1, e_words, e_scale
                 lhsT=w_q[0][:, P * t : P * (t + 1)].bitcast(FP8X4),
                 lhsT_scale=w_s[0][:, P * t : P * (t + 1)],
                 rhs=w_q[0][:, 0:width].bitcast(FP8X4),
-                rhs_scale=e_planes[:, 0, 0:width],
+                rhs_scale=w_s[0][:, 0:width],
                 start=True,
                 stop=True,
             )
 
+        h_acc = [bank(i, [P, PACK, TOK], "h_acc%d" % i) for i in range(TILES - 1)]
+        for o in range(PASSES):
+            for i in range(TILES - 1):
+                project(h_acc[i], i, o)
         round_h(nc.scalar.copy, 0, 0, TOK)
         round_h(nc.vector.tensor_copy, 1, 0, TOK)
         round_h(nc.scalar.copy, 2, 0, TOK)
+        h_acc.append(bank(0, [P, PACK, TOK], "h_acc_last"))
+        for o in range(PASSES):
+            project(h_acc[3], 3, o)
         round_h(nc.scalar.copy, 3, 0, TOK)
 
         h_codes = keep.tile([P, TILES, TOK], U32, name="h_codes", align_bytes=64)
@@ -266,7 +268,7 @@ def tile_picked_yhard_hinge_p_kernel(tc, x_words, x_scales, w1, e_words, e_scale
         nc.scalar.activation(out=excess[:], in_=gap[:], func=ACT.Relu)
         opened = {0: open_sums(pairs[:, 0, 0, 1], (4, 5)), 1: open_sums(best[:, 1], (6, 7))}
         turned = {1: close_sums(1, opened[1], [])}
-        turned[2] = close_sums(2, open_sums(best[:, 2], (0, 1)), [])
+        turned[2] = close_sums(2, open_sums(best[:, 2], (3, 1)), [])
         turned[0] = close_sums(0, opened[0], [excess[:]])
         finish_turned(1, nc.sync, *turned[1])
         finish_turned(2, nc.sync, *turned[2])

from contextlib import ExitStack

import concourse.mybir as mybir
from concourse.masks import make_identity

K, T, S, H, D, U = 1024, 2048, 512, 512, 4, 512
FLOPS = 2 * K * H * S + 2 * 2 * H * S * U

F32 = mybir.dt.float32
BF16 = mybir.dt.bfloat16
I32 = mybir.dt.int32
U32 = mybir.dt.uint32
U16 = mybir.dt.uint16
U8 = mybir.dt.uint8
FP8X4 = mybir.dt.float8_e4m3fn_x4
ALU = mybir.AluOpType
ACT = mybir.ActivationFunctionType

P = 128
PACK = 4
PASSES = K // (P * PACK)
TOK = 128
TILES = S // TOK
V = U // D
MARGIN = 0.3
DIRECT = 3
X_SLICES = ((0, 128), (128, 256), (256, 512))
WARM_UPS = (512, 256)
SCORE_BANK = ((4, 5, 6, 7), (2, 3, 1, 0))


def tile_picked_yhard_hinge_p_kernel(tc, x_words, x_scales, w1, e_words, e_scales, offs, pos, neg, out):
    nc = tc.nc
    with ExitStack() as ctx:
        lists = ctx.enter_context(tc.tile_pool(name="lists", bufs=1))
        keep = ctx.enter_context(tc.tile_pool(name="keep", bufs=1))
        shared = ctx.enter_context(tc.tile_pool(name="shared", bufs=1))
        psum = ctx.enter_context(tc.psum_pool(name="psum", bufs=1))

        def bank(b, shape, name):
            return psum.tile(shape, F32, name=name, tag="bank%d" % b)

        offs_t = lists.tile([P, S // 16], U16, name="offs_t")
        neg_t = lists.tile([P, U // 16], U16, name="neg_t")
        pos_t = lists.tile([P, U // 16], U16, name="pos_t")

        xs_all = shared.tile([P, T], U8, name="xs_all", offset=0, align_bytes=64)
        es_all = shared.tile([P, T], U8, name="es_all", offset=8192, align_bytes=64)
        planes = keep.tile([P, 2, S], U8, name="planes", align_bytes=64)
        nc.vector.memset(xs_all[:].bitcast(I32), 0)
        nc.gpsimd.memset(es_all[:].bitcast(I32), 0)
        nc.vector.memset(planes[:].rearrange("p a n -> p (a n)").bitcast(I32), 0)
        e_planes = keep.tile([P, 2, U], U8, name="e_planes", align_bytes=64)
        nc.vector.memset(e_planes[:].rearrange("p a n -> p (a n)").bitcast(I32), 0)

        identity = keep.tile([P, P], F32, name="identity")
        make_identity(nc, identity[:])

        w_raw = [keep.tile([P, PACK, H], F32, name="w_raw%d" % o) for o in range(PASSES)]

        def load_w(o):
            nc.sync.dma_start(out=w_raw[o][:], in_=w1[512 * o : 512 * (o + 1), :].rearrange("(p j) c -> p j c", j=PACK))

        def load_words(tile, words):
            nc.sync.dma_start(out=tile[:], in_=words.rearrange("p n t -> p (n t)").bitcast(I32))

        load_w(0)
        nc.sync.dma_start(offs_t[:], offs)
        nc.sync.dma_start(out=xs_all[0:P:4, :].bitcast(I32), in_=x_scales.rearrange("o q c -> q o c").bitcast(I32))
        nc.sync.dma_start(neg_t[:], neg)
        nc.sync.dma_start(out=es_all[0:P:8, :].bitcast(I32), in_=e_scales[0].bitcast(I32))
        nc.sync.dma_start(pos_t[:], pos)
        load_w(1)
        xw_all = [keep.tile([P, T], I32, name="xw_all0", tag="xw0", align_bytes=64)]
        load_words(xw_all[0], x_words[0])

        xs_g = shared.tile([P, S], U8, name="xs_g", offset=19456, align_bytes=64)
        es_g = shared.tile([P, 2, U], U8, name="es_g", offset=24576, align_bytes=64)
        nc.vector.tensor_copy(xs_g[:], xs_all[:].indirect(offs_t[:]))
        w_bf = [keep.tile([P, PACK, P, PACK], BF16, name="w_bf%d" % o, align_bytes=64) for o in range(PASSES)]

        def cast_w(o):
            nc.scalar.activation(
                out=w_bf[o][:].rearrange("p t m j -> p m t j"),
                in_=w_raw[o][:].rearrange("p j (m t) -> p m t j", t=PACK),
                func=ACT.Copy,
            )

        cast_w(0)
        for q in range(4):
            nc.sync.dma_start(
                out=planes[32 * q : 32 * q + 4].rearrange("p a n -> p (a n)").bitcast(I32),
                in_=xs_g[32 * q : 32 * q + 32 : 4, :].bitcast(I32),
            )
        xw_all.append(shared.tile([P, T], I32, name="xw_all1", offset=0, align_bytes=64))
        load_words(xw_all[1], x_words[1])
        ew_all = shared.tile([P, T], I32, name="ew_all", offset=8192, align_bytes=64)
        for side, picks in enumerate((neg_t, pos_t)):
            nc.vector.tensor_copy(es_g[:, side, :].rearrange("p (d v) -> p v d", d=D), es_all[:].indirect(picks[:]))
        load_words(ew_all, e_words[0])

        w_q = []
        w_s = []
        cast_w(1)

        def quantize_w(o, scales_offset):
            w_q.append(keep.tile([P, H], U32, name="w_q%d" % o, align_bytes=64))
            w_s.append(shared.tile([P, H], U8, name="w_s%d" % o, offset=scales_offset, align_bytes=64))
            nc.vector.quantize_mx(out=w_q[o][:].bitcast(FP8X4), scales=w_s[o][:], in_=w_bf[o][:].rearrange("p t m j -> p (t m j)"))

        quantize_w(0, 19968)
        for q in range(4):
            nc.sync.dma_start(
                out=e_planes[32 * q : 32 * q + 4].rearrange("p a n -> p (a n)").bitcast(I32),
                in_=es_g[32 * q : 32 * q + 32 : 8, :, :].rearrange("p a n -> p (a n)").bitcast(I32),
            )
        xw_g = [keep.tile([P, S], U32, name="xw_g%d" % o, align_bytes=64) for o in range(PASSES)]

        def gather_x(o):
            for lo, hi in X_SLICES:
                nc.vector.tensor_copy(xw_g[o][:, lo:hi], xw_all[o][:].bitcast(U32).indirect(offs_t[:, lo // 16 : hi // 16]))

        gather_x(0)
        quantize_w(1, 19456)
        gather_x(1)

        h_bf0 = keep.tile([P, 1, TOK, PACK], BF16, name="h_bf0", align_bytes=64)
        h_bf1 = keep.tile([P, 1, TOK, PACK], BF16, name="h_bf1", align_bytes=64)
        h_bf23 = keep.tile([P, 2, TOK, PACK], BF16, name="h_bf23", align_bytes=64)
        h_bf = [h_bf0[:, 0], h_bf1[:, 0], h_bf23[:, 0], h_bf23[:, 1]]

        def project(acc, i, o):
            for t in range(PACK):
                ch = slice(P * t, P * (t + 1))
                nc.tensor.matmul_mx(
                    out=acc[:, t, :],
                    lhsT=w_q[o][:, ch].bitcast(FP8X4),
                    lhsT_scale=w_s[o][:, ch],
                    rhs=xw_g[o][:, TOK * i : TOK * (i + 1)].bitcast(FP8X4),
                    rhs_scale=planes[:, o, TOK * i : TOK * (i + 1)],
                    start=(o == 0 and t == 0),
                    stop=(o == PASSES - 1 and t == PACK - 1),
                )

        def round_h(copy, i, lo, hi):
            copy(out=h_bf[i][:, lo:hi], in_=h_acc[i][:, :, lo:hi].rearrange("p t n -> p n t"))

        for t, width in enumerate(WARM_UPS):
            idle = bank(4 + t, [P, width], "idle")
            nc.tensor.matmul_mx(
                out=idle[:],
                lhsT=w_q[0][:, P * t : P * (t + 1)].bitcast(FP8X4),
                lhsT_scale=w_s[0][:, P * t : P * (t + 1)],
                rhs=w_q[0][:, 0:width].bitcast(FP8X4),
                rhs_scale=w_s[0][:, 0:width],
                start=True,
                stop=True,
            )

        h_acc = [bank(i, [P, PACK, TOK], "h_acc%d" % i) for i in range(TILES - 1)]
        for o in range(PASSES):
            for i in range(TILES - 1):
                project(h_acc[i], i, o)
        round_h(nc.scalar.copy, 0, 0, TOK)
        round_h(nc.vector.tensor_copy, 1, 0, TOK)
        round_h(nc.scalar.copy, 2, 0, TOK)
        h_acc.append(bank(0, [P, PACK, TOK], "h_acc_last"))
        for o in range(PASSES):
            project(h_acc[3], 3, o)
        round_h(nc.scalar.copy, 3, 0, TOK)

        h_codes = keep.tile([P, TILES, TOK], U32, name="h_codes", align_bytes=64)
        h_scales01 = keep.tile([P, 2, TOK], U8, name="h_scales01", align_bytes=64)
        h_scales23 = shared.tile([P, 2, TOK], U8, name="h_scales23", offset=24576, align_bytes=64)
        h_q = [h_codes[:, i] for i in range(TILES)]
        h_s = [h_scales01[:, 0], h_scales01[:, 1], h_scales23[:, 0], h_scales23[:, 1]]

        def quantize_h(codes, scales, values):
            nc.vector.quantize_mx(
                out=codes.rearrange("p i n -> p (i n)").bitcast(FP8X4),
                scales=scales.rearrange("p i n -> p (i n)"),
                in_=values[:].rearrange("p i n t -> p (i n t)"),
            )

        quantize_h(h_codes[:, 0:1], h_scales01[:, 0:1], h_bf0)
        quantize_h(h_codes[:, 1:2], h_scales01[:, 1:2], h_bf1)
        nw_g = keep.tile([P, U], U32, name="nw_g", align_bytes=64)
        nc.vector.tensor_copy(nw_g[:].rearrange("p (d v) -> p v d", d=D), ew_all[:].bitcast(U32).indirect(neg_t[:]))
        quantize_h(h_codes[:, 2:4], h_scales23[:], h_bf23)
        pw_g = shared.tile([P, U], U32, name="pw_g", offset=25088, align_bytes=64)
        nc.vector.tensor_copy(pw_g[:].rearrange("p (d v) -> p v d", d=D), ew_all[:].bitcast(U32).indirect(pos_t[:]))

        def scores(lhsT, lhsT_scale, rhs, rhs_scale, acc):
            nc.tensor.matmul_mx(
                out=acc,
                lhsT=lhsT.bitcast(FP8X4),
                lhsT_scale=lhsT_scale,
                rhs=rhs.bitcast(FP8X4),
                rhs_scale=rhs_scale,
                start=True,
                stop=True,
            )

        def add_turned(acc, values, start, stop):
            nc.tensor.matmul(acc, lhsT=values, rhs=identity[:], is_transpose=True, start=start, stop=stop)

        sides = ((nw_g, 0), (pw_g, 1))
        pairs = keep.tile([P, TILES, 2, 2, V], F32, name="pairs")
        best = keep.tile([P, TILES, V], F32, name="best")

        def first_round(i, side):
            words, plane = sides[side]
            acc = bank(SCORE_BANK[side][i], [P, D, V], "s_acc")
            if i != DIRECT:
                for d in range(D):
                    cols = slice(V * d, V * (d + 1))
                    scores(words[:, cols], e_planes[:, plane, cols], h_q[i], h_s[i], acc[:, d])
            else:
                scores(h_q[i], h_s[i], words[:], e_planes[:, plane, :], acc[:].rearrange("p d v -> p (d v)"))
            upper = keep.tile([P, 2, V], F32, name="upper%d_%d" % (i, side))
            if side == 0:
                nc.scalar.activation(out=upper[:], in_=acc[:, 2:4], func=ACT.Copy, bias=MARGIN)
                nc.vector.scalar_tensor_tensor(out=pairs[:, i, side], in0=acc[:, 0:2], scalar=MARGIN, in1=upper[:], op0=ALU.add, op1=ALU.max)
            else:
                nc.scalar.activation(out=upper[:], in_=acc[:, 2:4], func=ACT.Copy, scale=-1.0)
                nc.vector.scalar_tensor_tensor(out=pairs[:, i, side], in0=acc[:, 0:2], scalar=-1.0, in1=upper[:], op0=ALU.mult, op1=ALU.max)

        gap = keep.tile([P, V], F32, name="gap")

        def best_negatives(lo, hi):
            nc.vector.tensor_tensor(out=best[:, lo:hi], in0=pairs[:, lo:hi, 0, 0], in1=pairs[:, lo:hi, 0, 1], op=ALU.max)

        def open_sums(term, banks):
            accs = [bank(b, [P, V], "turned") for b in banks]
            for acc in accs:
                add_turned(acc[:], term, True, False)
            return accs

        def close_sums(i, accs, more_terms):
            for half in range(2):
                for term in more_terms:
                    add_turned(accs[half][:], term, False, False)
                add_turned(accs[half][:], pairs[:, i, 1, half], False, True)
            clipped = keep.tile([P, V], F32, name="clipped%d" % i)
            nc.scalar.activation(out=clipped[:], in_=accs[0][:], func=ACT.Relu)
            return accs[1], clipped

        loss = keep.tile([P, TILES, V], F32, name="loss")
        sums = keep.tile([P, 2, V], F32, name="sums")

        def store(i, queue):
            queue.dma_start(out=out[TOK * i : TOK * (i + 1), :], in_=loss[:, i])

        def finish_turned(i, queue, acc, clipped):
            nc.vector.tensor_tensor(out=loss[:, i], in0=acc[:], in1=clipped[:], op=ALU.max)
            store(i, queue)

        for i in range(TILES):
            first_round(i, 0)
        nc.gpsimd.tensor_tensor(out=gap[:], in0=pairs[:, 0, 0, 0], in1=pairs[:, 0, 0, 1], op=ALU.subtract)
        best_negatives(1, 3)
        first_round(1, 1)
        first_round(2, 1)
        first_round(0, 1)
        best_negatives(3, 4)
        first_round(3, 1)
        excess = shared.tile([P, V], F32, name="excess", offset=25088, align_bytes=64)
        nc.scalar.activation(out=excess[:], in_=gap[:], func=ACT.Relu)
        opened = {0: open_sums(pairs[:, 0, 0, 1], (4, 5)), 1: open_sums(best[:, 1], (6, 7))}
        turned = {1: close_sums(1, opened[1], [])}
        turned[2] = close_sums(2, open_sums(best[:, 2], (3, 1)), [])
        turned[0] = close_sums(0, opened[0], [excess[:]])
        finish_turned(1, nc.sync, *turned[1])
        finish_turned(2, nc.sync, *turned[2])
        nc.vector.tensor_tensor(out=sums[:], in0=pairs[:, 3, 1], in1=best[:, 3:4].to_broadcast([P, 2, V]), op=ALU.add)
        finish_turned(0, nc.scalar, *turned[0])
        nc.vector.scalar_tensor_tensor(out=loss[:, 3], in0=sums[:, 0], scalar=0.0, in1=sums[:, 1], op0=ALU.max, op1=ALU.max)
        store(3, nc.sync)
